import numpy as np, ml_dtypes
CORES = [48,51,52,55]
N = 4
import mx_ref
BF = ml_dtypes.bfloat16
def gentries(a):
    return np.ascontiguousarray(a.reshape(8, 16, -1).transpose(0, 2, 1)).reshape(8, -1)
def gtable(e):
    e = np.asarray(e); return np.ascontiguousarray(e.reshape(8, -1, 16).transpose(0, 2, 1)).reshape(128, -1).astype(np.int32)
def gcols(t, e):
    v = np.concatenate([t.reshape(8, 16, -1, 4), np.zeros((8, 16, 1, 4), BF)], axis=2)
    return np.ascontiguousarray(np.stack([v[g][:, e[g]] for g in range(8)])).reshape(128, -1)
def tile(rs):
    return np.stack(rs, axis=2).reshape(128, -1).astype(BF)
def pick(q, e):
    c = np.concatenate([q[0].reshape(128, -1, 4), np.zeros((128, 1, 4), np.uint8)], axis=1); s = np.concatenate([q[1], np.ones((16, 1), np.uint8)], axis=1)
    return (np.ascontiguousarray(c[:, e].reshape(128, -1)), np.ascontiguousarray(s[:, e]))
def join(*qs):
    return (np.concatenate([q[0] for q in qs], axis=1), np.concatenate([q[1] for q in qs], axis=1))
def put(q, e, v):
    c, s = q[0].reshape(128, -1, 4).copy(), q[1].copy(); c[:, e] = v[0].reshape(128, -1, 4); s[:, e] = v[1]
    return (c.reshape(128, -1), s)
def pk(c, s):
    return (np.ascontiguousarray(c), mx_ref.live(s))
def emit(q):
    return q[0], q[1]
def packed(v, rng):
    q = [mx_ref.quantize(np.ascontiguousarray(v[r])) for r in range(N)]
    return np.stack([a for a, b in q]), np.stack([mx_ref.plane(b, rng) for a, b in q])
def values_of_codes():
    e, c = np.zeros((128, 128, 4), np.float32), np.zeros((128, 2, 4), np.uint8)
    e[np.arange(128), np.arange(128), 0] = 1
    c[:127, :, 0] = np.arange(256).reshape(2, 128).T[:127]
    return mx_ref.matmul(mx_ref.quantize(e.reshape(128, 512).astype(BF)), (c.reshape(128, 8), np.full((16, 2), 127, np.uint8))).T.reshape(-1).astype(np.float64)
CODE_VALUE, SCALE_VALUE = values_of_codes(), 2.0 ** (np.arange(256) - 127.0)
def decode(q):
    return (CODE_VALUE[q[0]].reshape(16, 8, -1, 4) * SCALE_VALUE[q[1]][:, None, :, None] + 0.0).reshape(128, -1).astype(np.float32)
def f(rng, *shape):
    return mx_ref.flush((rng.standard_normal(shape, dtype=np.float32) * np.exp2(rng.integers(-2, 3, shape[:-1] + (1,)))).astype(BF))
def wide(rng, *shape, cols=0):
    v = rng.standard_normal(shape, dtype=np.float32) * np.exp2(rng.integers(-12, 13, shape)).astype(np.float32)
    if cols: v *= np.repeat(np.exp2(rng.integers(-cols, cols + 1, shape[:-2] + (1, shape[-1] // 4))) * (rng.random(shape[:-2] + (1, shape[-1] // 4)) > 0.0625), 4, axis=-1).astype(np.float32)
    return mx_ref.flush(v.astype(BF))
C, H, R = 384, 48, 2
def score(a, b):
    e = np.zeros((8, 16, 8, 16, 4), np.float32)
    for g in range(8): e[g, :, g] = 1
    z = (a.astype(np.float32) * b.astype(np.float32)).astype(BF)
    return mx_ref.matmul(mx_ref.quantize(e.reshape(128, 512).astype(BF)), mx_ref.quantize(z))[::16] + np.float32(0.0)
def big(v, k, low):
    v = v.astype(np.float32) * np.float32(k)
    v[np.abs(v) < np.float32(low)] = 0
    return v.astype(BF)
def state(rng):
    return big(f(rng, N, 128, 4 * C), 16, 2.0 ** -12)
def any_lists(rng):
    return rng.integers(0, C, (N, 8, 2, C)), rng.integers(0, N * H, (N, 8, C))
def unit():
    w = np.zeros((128, 4, 128, 4), np.float32)
    i = np.arange(128)
    for b in range(4): w[i, b, i, b] = 32
    return w.reshape(128, 2048).astype(BF)
def pack(rng, x, a, b, k=1, still=None):
    w = big(f(rng, N, 128, 2048), k, 2.0 ** -16)
    if still is not None: w[still] = unit()
    c, p = packed(w, rng)
    return {"x": x, "c1": np.stack([gtable(e.reshape(8, 2 * C)) for e in a]), "c2": np.stack([gtable(e) for e in b]), "v": np.array(f(rng, N, 128, 512)), "wc": c, "ws": p}
def signs(rng):
    return np.stack([rng.permutation(8) % 2 * 2.0 - 1.0 for r in range(N)])
def halves(rng):
    a, b = any_lists(rng)
    q, k, w = [np.zeros((N, 8, C // 2), int) for i in range(3)]
    for r in range(N):
        for g in range(8):
            o = rng.permutation(C)
            q[r, g], k[r, g] = o[:C // 2], o[C // 2:]
            c = 2 * rng.permutation(C // 4)[:H] + 1
            w[r, g] = rng.permutation(np.concatenate([c, c, c, rng.choice(c, C // 2 - 3 * H)]))
            i = rng.permutation(C // 2) % 2
            for n in range(2):
                a[r, g, n, q[r, g]] = k[r, g][np.where(i == n, w[r, g], w[r, g] - 1)]
                a[r, g, n, k[r, g]] = rng.permutation(q[r, g])
    return a, b, q, k, w
def setup_inputs(rng):
    a, b = any_lists(rng)
    return pack(rng, state(rng), a, b)
def setup_inputs_ties(rng):
    x = state(rng)
    e = rng.permutation(N)
    for r in range(N):
        k = np.zeros(C, int) if r == e[0] else rng.permutation(C) % 3
        t = x[r].reshape(128, C, 4)[:, :3].copy()
        t[:, 2] = 0
        x[r] = t[:, k].reshape(128, 4 * C)
    x[e[1]] = 0
    a, b = any_lists(rng)
    return pack(rng, x, a, b)
def setup_inputs_near(rng):
    a, b, q, k, w = halves(rng)
    s = signs(rng)
    d = ((np.arange(C // 2)[:, None] >> np.arange(8)) & 1) * np.exp2(np.arange(8) - 12.0)
    x = np.zeros((N, 8, 16, C, 4))
    z = np.zeros((8, N * H), int)
    for r in range(N):
        for g in range(8):
            m, i, j = rng.integers(4, 8, (13, C // 2, 4)) * rng.choice([-1.0, 1.0], (13, C // 2, 4)), q[r, g], k[r, g]
            p = x[r, g]
            p[0, i, 0] = s[r, g]
            p[0, j, 0] = 1
            p[8:10, i] = 2.0 ** -11
            p[8, j] = d[:, :4]
            p[9, j] = d[:, 4:]
            p[1:4, i] = m[:3] * 0.25
            p[4:8, j] = m[3:7] * 0.25
            p[10:13, i] = m[7:10] * 2.0 ** -9
            p[13:16, j] = m[10:] * 2.0 ** -9
            t, n = np.zeros(C, int), np.zeros(C, int)
            t[i] = j[w[r, g]]
            t[j] = a[r, g, 0, j]
            n[j] = np.arange(C // 2)
            z[g, H * r:H * r + H] = n[np.argsort(-np.bincount(t, minlength=C), kind="stable")[:H]]
    for g in range(8):
        o = np.argsort(z[g], kind="stable")
        t = np.argsort(o)
        for r in range(N): b[r, g, q[r, g]] = o[t[b[r, g, k[r, g][w[r, g]]]] ^ 1]
    return pack(rng, x.astype(np.float32).reshape(N, 128, 4 * C).astype(BF), a, b)
def setup_inputs_huge(rng):
    a, b, q, k, w = halves(rng)
    s = signs(rng)
    c = int(rng.integers(N))
    s[c] = 1
    b = rng.choice(np.flatnonzero(np.arange(N * H) // H != c), (N, 8, C))
    x = np.zeros((N, 8, 16, C, 4))
    odd = np.arange(C // 2) % 2 == 1
    for r in range(N):
        for g in range(8):
            x[r, g][:, q[r, g]] = s[r, g] * (1 + 0.25 * rng.random((16, C // 2, 4)))
            x[r, g][:, k[r, g]] = np.where(odd == (s[r, g] > 0), 1.5, 1.0)[None, :, None] + 0.25 * rng.random((16, C // 2, 4))
    x[c] *= -(2.0 ** -26)
    for g in range(8):
        i = np.concatenate([q[c, g], k[c, g][np.arange(C // 2) % 4 < 2]])
        b[c, g, i] = H * c + rng.integers(0, H, len(i))
    return pack(rng, (x * 2.0 ** 14).astype(np.float32).reshape(N, 128, 4 * C).astype(BF), a, b, 2.0 ** -3, c)
def setup_inputs_star(rng):
    a, b = any_lists(rng)
    e = rng.permutation(N)
    a[e[0]] = rng.integers(0, C, (8, 1, 1))
    b[e[0]] = rng.integers(0, N * H, (8, 1))
    for g in range(8):
        a[e[1], g] = rng.permutation(C)
        t, i = rng.permutation(C)[:2], rng.integers(0, 2, C)
        a[e[2], g, 0], a[e[2], g, 1] = t[i], t[1 - i]
    a[e[3]] = C - 1 - np.minimum(C - 1, (C * rng.random((8, 2, C)) ** 4).astype(int))
    b[e[1]] = H * e[1] + rng.integers(0, H, (8, C))
    b[e[2]] = H * e[3] + rng.integers(0, H, (8, C))
    return pack(rng, state(rng), a, b)
def setup_inputs_spread(rng):
    a, b = any_lists(rng)
    return pack(rng, big(wide(rng, N, 128, 4 * C, cols=2), 2.0 ** -3, 2.0 ** -12), a, b)
def check_inputs(d):
    b = []
    for k in ("x", "v"):
        a = np.abs(d[k].astype(np.float32))
        if not (np.isfinite(a).all() and ((a == 0) | (a >= 2.0 ** -30) & (a <= 2.0 ** 30)).all()): b.append("a value of " + k)
    for k, n in (("c1", C), ("c2", N * H)):
        if not ((d[k] >= 0) & (d[k] < n)).all(): b.append("an entry of " + k)
    if ((d["wc"] & 127) == 127).any(): b.append("a code of wc")
    s = np.stack([mx_ref.live(p) for p in d["ws"]])
    if not ((s >= 1) & (s <= 157)).all(): b.append("a scale of ws")
    return b
def reference(x, c1, c2, v, wc, ws):
    now = [x[r] for r in range(N)]
    hl = np.zeros((N, 8, R * H), np.float32)
    for t in range(R):
        points, hubs = [], []
        for r in range(N):
            e = gentries(c1[r])
            e0, e1 = e[:, :C], e[:, C:]
            p = np.where(score(now[r], gcols(now[r], e1)) > score(now[r], gcols(now[r], e0)), e1, e0)
            n = np.stack([np.bincount(p[g], minlength=C) for g in range(8)])
            h = np.argsort(-n, axis=1, kind="stable")[:, :H]
            points.append(p)
            hubs.append(mx_ref.quantize(gcols(now[r], h)))
            hl[r, :, H * t:H * t + H] = h
        slots = decode(join(*hubs)).astype(BF)
        for r in range(N):
            a0 = gentries(c2[r])
            a1 = np.take_along_axis(a0, points[r], axis=1)
            a = np.where(score(now[r], gcols(slots, a1)) > score(now[r], gcols(slots, a0)), a1, a0)
            m = ((now[r].astype(np.float32) + gcols(slots, a).astype(np.float32)) * np.float32(0.5)).astype(BF)
            q, w = mx_ref.quantize(m), pk(wc[r], ws[r])
            now[r] = tile([mx_ref.matmul(pick(w, np.arange(128 * b, 128 * b + 128)), q) * np.float32(0.03125) for b in range(4)])
    y = np.zeros((N, 128, C), np.float32)
    oc, osc = np.zeros((N, 128, 4 * C), np.uint8), np.zeros((N, 16, C), np.uint8)
    for r in range(N):
        q = mx_ref.quantize(now[r])
        y[r] = mx_ref.matmul(mx_ref.quantize(v[r]), q)
        oc[r], osc[r] = emit(q)
    return {"y": y, "hl": hl, "oc": oc, "osc": osc}

@@ -1,0 +1,516 @@
+from concourse.bass import DstId, RemoteDMATransfer
+from concourse.mybir import dt, AluOpType, ActivationFunctionType
+
+C, H, R, N = 384, 48, 2, 4
+S_ = N * H
+LV = 8
+KB = 64
+BIG = 1e29
+CH = ((0, 256), (256, 384))
+SP, SC, SM = ((0, 0), (0, 0)), (0, 0), 0
+
+BF, F32, I32, U16, Q8, U8 = "bfloat16", "float32", "int32", "uint16", "float8_e4m3fn_x4", "uint8"
+_B = {
+    BF: "x0 xp xh xi xq z0 z1 tg0 tg1 mm fh cst:1536 vt bb zb:512 wn:480 gg:2304 dd:1024 o128 n128 t128 d128:128 ee:2048 "
+        "i16 m16 h16 r16 e2 fs2 fl am aw:384 r64 cmp cs:256 eq fp c2r:768",
+    F32: "ysb nc nu e1 fs:384 pf:12 lev one sa va:192 plc tbl:400 zer:4 v1:96 v2 hm hw:48 km kw hh0 hh1:64 "
+         "v3 c2a c2b a0 a0p c0p da db pw af:24",
+    I32: "l1 lo hi:48 l2:24 pi:1 pa:4 key kk:384 kp:64",
+    U16: "og:144 o1:192 o1p:48 olb:12 onw:2 nw:32 ork oa0 op oa1 oa:24 or2 oh:4",
+    Q8: "qz:768 qm qx qk:384 qw qc qe:512 qv:128 qd:256 qq:192 lq0 lq1:272",
+    U8: "sz:768 sm sx sk:384 sw sc se:512 sv:128 sd:256 sq:192 ls0 ls1:272",
+}
+SCRATCH = {"vals": ("sbuf", [128, 6, 3, 8], F32), "gt": ("sbuf", [128, 4, 768], BF), "tt": ("sbuf", [128, 4, 768], BF)}
+for _d, _text in _B.items():
+    _names = []
+    for _w in _text.split():
+        _names.append(_w.split(":")[0])
+        if ":" in _w:
+            for _n in _names:
+                SCRATCH[_n] = ("sbuf", [128, int(_w.split(":")[1])], _d)
+            _names = []
+for _i in range(8):
+    SCRATCH["ps%d" % _i] = ("psum", [128, 512], F32)
+POOL = {"s": 132, "d": 14}
+SEMAPHORES = ["%s%d" % (_k, _i) for _k in POOL for _i in range(POOL[_k])] + ["arr0", "arr1", "sent"]
+
+
+def _emit(ops, queues, T):
+    last_w, readers, known, groups, before = {}, {}, {}, {}, {}
+    for i, o in enumerate(ops):
+        groups.setdefault(o["grp"], []).append(i)
+    for i, o in enumerate(ops):
+        deps = set()
+        for k in o["r"]:
+            deps.update(last_w.get(k, ()))
+        for k in o["w"]:
+            held = before.setdefault((o["grp"], k), set())
+            held.update(last_w.get(k, ()))
+            held.update(readers.get(k, ()))
+            deps.update(held)
+        if o["eng"] == "P":
+            deps = set(d for d in deps if ops[d]["eng"] != "P")
+        kn = known.setdefault(o["eng"], set())
+        need = set(ops[d]["grp"] for d in deps if ops[d]["grp"] != o["grp"])
+        o["waits"] = []
+        for gr in sorted(need, key=lambda a: -groups[a][-1]):
+            if gr in kn:
+                continue
+            assert groups[gr][-1] < i, ("group not complete", gr, o["grp"])
+            o["waits"].append(gr)
+            kn.add(gr)
+            for m in groups[gr]:
+                kn |= ops[m]["kn"]
+        o["kn"] = set(kn)
+        for k in o["r"]:
+            readers.setdefault(k, []).append(i)
+        for k in o["w"]:
+            last_w[k] = [d for d in last_w.get(k, ()) if ops[d]["grp"] == o["grp"]] + [i]
+            readers[k] = [d for d in readers.get(k, ()) if ops[d]["grp"] == o["grp"]]
+    used = set(gr for o in ops for gr in o["waits"])
+    sem, count, owner, nxt = {}, {}, {}, {"s": 0, "d": 0}
+    for i, o in enumerate(ops):
+        gr = o["grp"]
+        if gr in used and gr not in sem:
+            if o["fixed"]:
+                sem[gr] = o["fixed"]
+                continue
+            pool = "d" if o["inc"] == 16 else "s"
+            while True:
+                s = "%s%d" % (pool, nxt[pool] % POOL[pool])
+                nxt[pool] += 1
+                if all(p in ops[m]["kn"] for p in owner.get(s, ()) for m in groups[gr]):
+                    break
+            owner.setdefault(s, []).append(gr)
+            count[s] = count.get(s, 0) + sum(ops[m]["inc"] for m in groups[gr])
+            sem[gr] = (s, count[s])
+    for o in ops:
+        q = queues[o["eng"]]
+        for gr in o["waits"]:
+            q.wait_ge(T.sem[sem[gr][0]], sem[gr][1])
+        if o["fn"] is not None:
+            ins = o["fn"]()
+            if o["grp"] in used and not o["fixed"]:
+                ins.then_inc(T.sem[sem[o["grp"]][0]], o["inc"])
+
+
+def rank_program(g, core, T, topo):
+    me = T.rank_of(core)
+    if me is None:
+        return
+    A, AF = AluOpType, ActivationFunctionType
+    V, S, P, Y = g.vector, g.scalar, g.tensor, g.sync
+    ops = []
+
+    def op(eng, fn, r=(), w=(), grp=None, inc=1, fixed=None):
+        ops.append({"eng": eng, "fn": fn, "r": list(r), "w": list(w), "inc": inc, "fixed": fixed,
+                    "grp": grp if grp is not None else "#%d" % len(ops)})
+
+    def ts(out, in0, s1, o0, r, w, s2=None, o1=None, grp=None):
+        if o1 is None:
+            op("V", lambda: V.tensor_scalar(out, in0, s1, None, o0), r, w, grp)
+        else:
+            op("V", lambda: V.tensor_scalar(out, in0, s1, s2, o0, o1), r, w, grp)
+
+    def tt(out, in0, in1, o, r, w, grp=None):
+        op("V", lambda: V.tensor_tensor(out, in0, in1, o), r, w, grp)
+
+    def cp(out, in_, r, w, grp=None):
+        op("V", lambda: V.tensor_copy(out, in_), r, w, grp)
+
+    def ms(ap, c, w, grp=None):
+        op("V", lambda: V.memset(ap, c), (), w, grp)
+
+    def scan(out, d0, d1, o0, o1, r, w):
+        op("V", lambda: V.tensor_tensor_scan(out, d0, d1, 0.0, o0, o1), r, w)
+
+    def qz(q, s, a, b, in_, r, w, grp=None):
+        op("V", lambda: V.quantize_mx(q[:, a:b], s[:, a:b], in_), r, w, grp)
+
+    def act(out, in_, r, w, scale=None, grp=None, bias=None, func=AF.Identity):
+        if bias is not None:
+            op("S", lambda: S.activation(out, in_, func, bias=bias, scale=scale), r, w, grp)
+        elif scale is None:
+            op("S", lambda: S.activation(out, in_, AF.Copy), r, w, grp)
+        else:
+            op("S", lambda: S.activation(out, in_, AF.Copy, scale=scale), r, w, grp)
+
+    def mx(bank, lq, ls, a, rq, rs, b, n, start, stop, r, grp=None):
+        op("P", lambda: P.matmul_mx(T["ps%d" % bank][:, 0:n], lq[:, a:a + 128], ls[:, a:a + 128],
+                                    rq[:, b:b + n], rs[:, b:b + n], start, stop), r, ["ps%d" % bank], grp)
+
+    def dma(eng, out, in_, r, w, grp=None):
+        op(eng, lambda: (Y if eng == "Y" else S).dma_start(out, in_), r, w, grp, 16)
+
+    def gp(fn, r, w):
+        op("G", fn, r, w)
+
+    def iota(out, pattern, base, r, w):
+        gp(lambda: g.iota(out, pattern, base, 0, allow_small_or_imprecise_dtypes=True), r, w)
+
+    def ps(b, n):
+        return T["ps%d" % b][:, 0:n]
+
+    def u8(ap):
+        return ap.bitcast(dt.uint8)
+
+    dma("Y", T.l1[:], T.c1[:], [], ["l1"])
+    dma("Y", T.x0[:], T.x[:], [], ["x0"])
+    dma("Y", T.l2[:], T.c2[:], [], ["l2"])
+
+    gp(lambda: g.iota(T.pi[:], [[0, 1]], 0, 1), [], ["pi"])
+    ms(T.o128[:], 1.0, ["o128"])
+    ms(T.wn[:, 0:160], 1.0, ["wn0"])
+    ms(T.zb[:], 0.0, ["zb"])
+    gp(lambda: g.affine_select(T.o128[:], T.o128[:], [[-16, 8], [0, 16]], A.is_ge, 0.0, 0, 1), ["o128"], ["o128"])
+    gp(lambda: g.affine_select(T.o128[:], T.o128[:], [[16, 8], [0, 16]], A.is_ge, 0.0, 15, -1), ["o128"], ["o128"])
+    gp(lambda: g.affine_select(T.wn[:, 0:160], T.wn[:, 0:160], [[-1, 160]], A.is_equal, 0.0, 16, 1), ["wn0"], ["wn0"])
+    ts(T.pa[:, 0:1], T.pi[:], 128 - 16, A.bitwise_and, ["pi"], ["pa"], grp="pa")
+    ts(T.pa[:, 1:2], T.pi[:], 15, A.bitwise_and, ["pi"], ["pa"], grp="pa")
+    ts(T.pa[:, 2:3], T.pi[:], 128 - 32, A.bitwise_and, ["pi"], ["pa"], grp="pa")
+    for a in range(4):
+        ms(T.gt[:, a, 3::4], 0.0, ["gt3"], "fill")
+    ms(T.dd[:, 3::4], 0.0, ["dd3"], "fill")
+    ms(T.zer[:], 0.0, ["zer"], "fill")
+    cp(T.pf[:, 0:3], T.pa[:, 0:3], ["pa"], ["pf"])
+    g16, pm = T.pf[:, 0:1], T.pf[:, 1:2]
+    act(T.eq[:, 0:512], T.zb[:], ["zb"], ["eq0"], grp="fs")
+    act(T.eq[:, 512:768], T.zb[:, 0:256], ["zb"], ["eq0"], grp="fs")
+    act(T.bb[:], T.zb[:], ["zb"], ["bb0"], grp="fs")
+    act(T.cst[:, 1024:1536], T.zb[:], ["zb"], ["cst2"], grp="fs")
+    act(T.one[:], T.zb[:, 0:192], ["zb"], ["one"], 1.0, "fs", 1.0)
+    ts(T.n128[:], T.o128[:], -1.0, A.mult, ["o128"], ["n128"])
+    for t in range(4):
+        cp(T.cst[:, t:512:4], T.o128[:], ["o128"], ["cst0"], "cst0")
+    ts(T.cst[:, 512:1024], T.cst[:, 0:512], -1.0, A.mult, ["cst0"], ["cst1"])
+    ts(T.wn[:, 160:320], T.wn[:, 0:160], -1.0, A.add, ["wn0"], ["wn"], -BIG, A.mult, grp="wn")
+    ts(T.wn[:, 320:480], T.wn[:, 0:160], -1.0, A.add, ["wn0"], ["wn"], BIG, A.mult, grp="wn")
+    gp(lambda: g.affine_select(T.t128[:], T.n128[:], [[-1, 128]], A.is_gt, 0.0, 0, 1), ["n128"], ["t128"])
+    iota(T.i16[:], [[0, 24], [1, 16]], 0, [], ["i16"])
+    iota(T.plc[:], [[1, 400]], 0, [], ["plc"])
+    iota(T.lev[0:64, :], [[-1, LV], [0, 24]], LV - 1, [], ["lev"])
+    iota(T.lev[64:128, :], [[1, LV], [0, 24]], 0, ["lev", "plc", "i16", "t128", "wn0", "pi"], ["lev2"])
+
+    ts(T.lo[:], T.l1[:], 15, A.bitwise_and, ["l1"], ["lohi"], grp="lohi")
+    ts(T.hi[:], T.l1[:], 4, A.logical_shift_right, ["l1"], ["lohi"], grp="lohi")
+    ts(T.o1[:, 0:48], T.l1[:], 4.0, A.mult, ["l1"], ["o1"], grp="o1")
+    for y, (src, k, c) in enumerate(((T.lo, 0, 336), (T.lo, 1, 176), (T.hi, 0, 16), (T.hi, 0, 0), (T.hi, 1, 16), (T.hi, 1, 0))):
+        ts(T.vals[:, y], src[:, 24 * k:24 * k + 24], g16, A.add, ["lohi", "pf"], ["vals"], float(c), A.add, grp="vals")
+    ts(T.o1[:, 48:96], T.l1[:], 4.0, A.mult, ["l1"], ["o1"], 1.0, A.add, grp="o1")
+    for t in (1, 2, 0):
+        cp(T.og[:, 48 * t:48 * t + 48], T.vals[:, :, t, :], ["vals"], ["og%d" % t])
+    for t in range(2, 4):
+        ts(T.o1[:, 48 * t:48 * t + 48], T.l1[:], 4.0, A.mult, ["l1"], ["o1"], float(t), A.add, grp="o1")
+    for t in (1, 2):
+        act(T.gg[:, 768 * t:768 * t + 768], T.wn[:].indirect(T.og[:, 48 * t:48 * t + 48]), ["wn", "wn0", "og%d" % t], ["gg%d" % t])
+    cp(T.gg[:, 0:768], T.wn[:].indirect(T.og[:, 0:48]), ["wn", "wn0", "og0"], ["gg0"])
+
+    def turns(t):
+        for a in range(4):
+            op("V", lambda a=a: V.transpose(T.gt[:, a, t::4], T.gg[:, 768 * t + a:768 * t + 768:4]),
+               ["gg%d" % t, "gt3"], ["gt%d" % t], "tr%d" % t)
+
+    def shuffles():
+        for a in range(4):
+            dma("Y", T.tt[:, a, :], T.gt[32 * a:32 * a + 32, :, :], ["gt0", "gt1", "gt2", "gt3"], ["tt"], "tt")
+        dma("Y", u8(T.qw[:]), T.wc[:], ["tt"], ["qw"], "ldw")
+        dma("Y", T.sw[:], T.ws[:], [], ["qw"], "ldw")
+        dma("Y", T.vt[:], T.v[:], [], ["vt"])
+
+    def late_constants_a():
+        ts(T.pf[:, 8:9], T.pf[:, 2:3], 64.0, A.is_ge, ["pf"], ["pf8"], -64.0, A.mult)
+        ts(T.d128[:], T.wn[:, 16:144], -512.0, A.mult, ["wn0"], ["d128"])
+        ts(T.pf[:, 7:8], T.pf[:, 2:3], 3.0, A.mult, ["pf", "pf8"], ["pf7"], T.pf[:, 8:9], A.add)
+        ts(T.m16[:], T.i16[:], pm, A.is_equal, ["i16", "pf"], ["m16"], grp="m16")
+        ts(T.pf[:, 3:4], g16, T.pf[:, 7:8], A.add, ["pf", "pf7"], ["pf3"], pm, A.add, grp="pf3")
+        ts(T.pf[:, 4:5], pm, 8.0, A.is_ge, ["pf"], ["pf3"], grp="pf3")
+        tt(T.cst[:, 1024:1536:4], T.t128[:], T.d128[:], A.add, ["t128", "d128", "cst2"], ["cst3"])
+        ts(T.pf[:, 5:6], T.pf[:, 4:5], -40.0, A.mult, ["pf3"], ["pf5"], 32.0, A.add, grp="pf5")
+        ts(T.pf[:, 6:7], T.pf[:, 4:5], 16.0, A.mult, ["pf3"], ["pf5"], 8.0, A.add, grp="pf5")
+        ts(T.r16[:], T.i16[:], 0.0, A.is_gt, ["i16"], ["r16"], grp="m16")
+        qz(T.qk, T.sk, 256, 384, T.cst[:, 1024:1536], ["cst3", "cst2"], ["qk2"])
+        ts(T.olb[:, 0:12:3], T.zer[:], T.pf[:, 3:4], A.add, ["pf3", "zer"], ["olb"], grp="olb")
+        ts(T.olb[:, 1:12:3], T.zer[:], T.pf[:, 3:4], A.add, ["pf5", "zer"], ["olb"], T.pf[:, 5:6], A.add, grp="olb")
+        ts(T.olb[:, 2:12:3], T.zer[:], T.pf[:, 3:4], A.add, ["pf5", "zer"], ["olb"], T.pf[:, 6:7], A.add, grp="olb")
+        ts(T.onw[:, 0:1], T.pf[:, 3:4], 0.0, A.add, ["pf3"], ["onw"], grp="olb")
+        ts(T.onw[:, 1:2], T.pf[:, 3:4], 32.0, A.add, ["pf3"], ["onw"], grp="olb")
+
+    def late_constants_c():
+        ts(T.c2a[:], T.l2[:], float(S_ - H * (me + 1)), A.add, ["l2"], ["c2a"])
+        ts(T.c0p[:], T.l1[:, 0:24], float(C), A.add, ["l1"], ["c0p"])
+        ts(T.c2b[:], T.c2a[:], float(S_), A.is_ge, ["c2a"], ["c2b"], -float(S_), A.mult)
+        cp(T.o1p[:], T.l1[:], ["l1"], ["o1p"])
+        tt(T.a0[:], T.c2a[:], T.c2b[:], A.add, ["c2a", "c2b"], ["a0"])
+        tt(T.e1[:, 15::16], T.l1[:, 24:48], T.c0p[:], A.subtract, ["l1", "c0p"], ["e1"])
+        cp(T.oa0[:], T.a0[:], ["a0"], ["oa0"], "oa0")
+        ts(T.a0p[:], T.a0[:], float(S_), A.add, ["a0"], ["a0p"], grp="oa0")
+
+    peers = [c for c in T.cores if c != core]
+    mask = topo.mask(core, peers[0])
+    for c in peers[1:]:
+        mask &= topo.mask(core, c)
+    lanes = bin(mask).count("1")
+    ids = [DstId(rid=topo.addr(c)[0], pnc=topo.addr(c)[1]) for c in peers]
+    spot = [H * ((me - T.rank_of(c) - 1) % N) for c in peers]
+    own = H * (N - 1)
+
+    def product(z, tg, a, b, win, wkey, off, other, okeys, alu, zk, split, name):
+        tk = lambda t: ["%s%d%s" % (tg.name, t, k[-1]) for k in zk]
+        ok = lambda t: [k if isinstance(k, str) else k(t) for k in okeys]
+        for t in range(4 - split, 4):
+            act(tg[:, C * t + a:C * t + b], win(t).indirect(off(t)), [wkey(t), okeys[0]], tk(t))
+        out = []
+        for t in range(4):
+            if t < 4 - split:
+                out.append(lambda t=t: tt(z[:, 4 * a + t:4 * b:4], win(t).indirect(off(t)), other(t), alu, [wkey(t)] + ok(t), zk, name))
+            else:
+                out.append(lambda t=t: tt(z[:, 4 * a + t:4 * b:4], tg[:, C * t + a:C * t + b], other(t), alu, tk(t) + ok(t)[1:], zk, name))
+        return out
+
+    def plane(buf, a, b):
+        return lambda t: buf[:, C * t + a:C * t + b]
+
+    xpk, xps = (lambda t: "xp%d" % t), ["xp%d" % t for t in range(4)]
+    for rd in range(R):
+        n_ = "r%d" % rd
+        last = rd == R - 1
+        if rd == 0:
+            turns(0)
+            qz(T.qk, T.sk, 0, 256, T.cst[:, 0:1024], ["cst0", "cst1"], ["qk"])
+            turns(1)
+            src, sk = (lambda t: T.x0[:, t::4]), (lambda t: "x0")
+            cp(T.xq[:, 0:C], src(0), ["x0"], ["xq0"])
+        else:
+            src, sk = plane(T.xp, 0, C), xpk
+        for t in range(1, 4):
+            act(T.xq[:, C * t:C * t + C], src(t), [sk(t)], ["xq%d" % t])
+        if rd == 0:
+            turns(2)
+            shuffles()
+        w = []
+        for k, (z, tg) in enumerate(((T.z0, T.tg0), (T.z1, T.tg1))):
+            zk = ["z%da" % k, "z%db" % k]
+            if rd == 0:
+                win, off = (lambda t: T.x0[:]), (lambda t, k=k: T.o1[:, 48 * t + 24 * k:48 * t + 24 * k + 24])
+            else:
+                win, off = plane(T.xp, 0, C), (lambda t, k=k: T.o1p[:, 24 * k:24 * k + 24])
+            w.append(product(z, tg, 0, C, win, sk, off, plane(T.xq, 0, C),
+                             ["o1" if rd == 0 else "o1p", lambda t: "xq%d" % t], A.mult, zk, SP[rd][k], n_ + "pz%d" % k))
+        for f in w[0]:
+            f()
+        w[1][0]()
+        qz(T.qz, T.sz, 0, C, T.z0[:], ["z0a", "z0b"], ["qz0"])
+        for f in w[1][1:]:
+            f()
+        for t in range(3):
+            mx(t, T.qz, T.sz, 128 * t, T.qk, T.sk, 128, 128, True, False, ["qz0", "qk"])
+        mx(3, T.qk, T.sk, 128, T.qz, T.sz, 0, C, True, False, ["qz0", "qk"])
+        q1 = (["qz1a"], ["qz1c"], ["qz1b"])
+        for t in range(3):
+            qz(T.qz, T.sz, C + 128 * t, C + 128 * t + 128, T.z1[:, 512 * t:512 * t + 512], ["z1a", "z1b"], q1[t])
+            mx(t, T.qz, T.sz, C + 128 * t, T.qk, T.sk, 0, 128, False, True, q1[t] + ["qk"])
+        mx(3, T.qk, T.sk, 0, T.qz, T.sz, C, C, False, True, ["qz1a", "qz1b", "qz1c", "qk"])
+        if rd == 0:
+            act(T.xp[:], T.xq[:], ["xq0", "xq1", "xq2", "xq3"], xps)
+            act(T.tbl[:], T.plc[:], ["plc"], ["tbl"], -512.0, None, float(C * 512))
+            act(T.e1[:], T.zb[:, 0:C], ["zb"], ["e1"], 1.0, None, 1.0)
+            late_constants_a()
+            for a in range(4):
+                qz(T.qc, T.sc, 128 * a, 128 * a + 128, T.tt[:, a, 256:768], ["tt"], ["qc"], "qc")
+        else:
+            act(T.xh[:], T.xp[:], xps, ["xh"], 0.5)
+        for k, alu in enumerate((A.is_le, A.is_gt)):
+            for t in range(3):
+                tt(T.dd[:, 512 * k + t:512 * k + 512:4], ps(t, 128), T.tt[:, :, 128 * k + t:128 * k + 128:4], alu,
+                   ["tt"], ["dd%d" % k, "ps%d" % t], n_ + "dd%d" % k)
+            qz(T.qd, T.sd, 128 * k, 128 * k + 128, T.dd[:, 512 * k:512 * k + 512], ["dd%d" % k, "dd3"], ["qd%d" % k])
+            mx(7, T.qd, T.sd, 128 * k, T.qc, T.sc, 256 + 64 * k, 192, k == 0, k == 1, ["qd%d" % k, "qc"])
+            mx(4, T.qd, T.sd, 128 * k, T.qc, T.sc, 64 * k, 192, k == 0, k == 1, ["qd%d" % k, "qc"])
+        if rd == 0:
+            ts(T.h16[:], T.i16[:], pm, A.not_equal, ["i16", "pf"], ["h16"], BIG, A.mult)
+            ms(T.r64[:], 1.0, ["r64"])
+        else:
+            tt(T.fl[:], ps(3, C), T.h16[:], A.is_gt, ["h16"], ["fla", "flb", "ps3"])
+        ts(T.nc[:, 0:192], ps(4, 192), float(LV - 1), A.min, [], ["nc", "ps4"])
+        act(T.nc[:, 192:384], ps(7, 192), [], ["nc2", "ps7"], -1.0, None, float(LV - 1), AF.Relu)
+        act(T.nu[:, 192:384], ps(7, 192), [], ["nu", "ps7"], grp=n_ + "nu")
+        act(T.nu[:, 0:192], ps(4, 192), [], ["nu", "ps4"], grp=n_ + "nu")
+        if rd == 0:
+            ms(T.r64[:, 0::64], 0.0, ["r64"])
+            act(T.e2[:], T.zb[:, 0:C], ["zb"], ["e2"], 1.0, None, 1.0)
+            act(T.xh[:], T.xp[:], xps, ["xh"], 0.5)
+            for b in range(4):
+                act(T.ee[:, 512 * b:512 * b + 512], T.zb[:], ["zb"], ["ee"], grp="ee")
+            for b in range(4):
+                act(T.ee[:, 512 * b + b:512 * b + 512:4], T.wn[:, 16:144], ["wn0", "ee"], ["ee1"], grp="ee1")
+        tt(T.eq[:, 0::4], T.nc[:].indirect(T.olb[:]), T.lev[:], A.is_equal, ["nc", "nc2", "olb", "lev", "lev2", "eq0"], ["eq"])
+        qz(T.qq, T.sq, 0, 192, T.eq[:], ["eq", "eq0"], ["qq"])
+        mx(5, T.qk, T.sk, 0, T.qq, T.sq, 0, 192, True, True, ["qq", "qk"])
+        mx(6, T.qk, T.sk, 256, T.qq, T.sq, 0, 192, True, True, ["qq", "qk2"])
+        cp(T.nw[:], T.nu[:].indirect(T.onw[:]), ["nu", "onw"], ["nw"])
+        scan(T.sa[:], T.one[:], ps(5, 192), A.mult, A.add, ["one"], ["sa", "ps5"])
+        third = C // 3
+
+        def keys(i):
+            tt(T.key[:, third * i:third * i + third], T.tbl[:].indirect(T.nw[:, 8 * i:8 * i + 8]), T.plc[:, third * i:third * i + third],
+               A.add, ["tbl", "nw", "plc"], ["key"], n_ + "key")
+
+        keys(0)
+        tt(T.va[:], T.sa[:], ps(6, 192), A.add, ["sa"], ["va", "ps6"])
+        keys(1)
+        tt(T.v1[:], T.va[:, 0:96], T.va[:, 96:192], A.min, ["va"], ["v1"])
+        keys(2)
+        tt(T.v2[:], T.v1[:, 0:48], T.v1[:, 48:96], A.min, ["v1"], ["v2"])
+        tt(T.v3[:], T.v2[:, 0:24], T.v2[:, 24:48], A.min, ["v2"], ["v3"])
+        ts(T.ork[:], T.v3[:], 511.0, A.add, ["v3"], ["ork"])
+        cp(T.kk[:].indirect(T.ork[:]), T.key[:], ["ork", "key"], ["kk"])
+        hh = T["hh%d" % rd]
+        tt(T.km[:], T.kk[:, 0:KB], T.m16[:, 0:KB], A.mult, ["kk", "m16"], ["km"])
+        ts(T.kp[:], T.kk[:, 0:KB], 511, A.bitwise_and, ["kk"], ["kp"])
+        scan(T.kw[:], T.r16[:, 0:KB], T.km[:], A.mult, A.add, ["r16", "km"], ["kw"])
+        for m in range(4):
+            ts(T.cmp[:, KB * m:KB * m + KB], T.kk[:, 0:KB], T.kw[:, 16 * m + 15:16 * m + 16], A.is_lt, ["kk", "kw"], ["cmp"], grp=n_ + "cmp")
+        scan(T.cs[:], T.r64[:], T.cmp[:], A.mult, A.add, ["r64", "cmp"], ["cs"])
+        cp(T.or2[:], T.cs[:, KB - 1::KB], ["cs"], ["or2"])
+        cp(hh[:].indirect(T.or2[:]), T.kp[:], ["or2", "kp"], ["hh%d" % rd])
+        tt(T.hm[:], hh[:, 0:H], T.m16[:, 0:H], A.mult, ["hh%d" % rd, "m16"], ["hm"])
+        scan(T.hw[:], T.r16[:, 0:H], T.hm[:], A.mult, A.add, ["r16", "hm"], ["hw"])
+        cp(T.oh[:, 0:3], T.hw[:, 15::16], ["hw"], ["oh"])
+        for t in range(4):
+            cp(T.bb[:, t:4 * H:4], T.xp[:, C * t:C * t + C].indirect(T.oh[:, 0:3]), [xpk(t), "oh", "bb0"], ["bb"], n_ + "bb")
+        lq, ls = T["lq%d" % rd], T["ls%d" % rd]
+        qz(lq, ls, own, own + 128, T.bb[:], ["bb", "bb0"], ["own%d" % rd])
+        for buf, view in ((lq, u8), (ls, lambda ap: ap)):
+            op("G", lambda buf=buf, view=view, rd=rd: g.remote_dma_fused([RemoteDMATransfer(
+                dst_ids=ids, dma_engine_mask=mask, remote_sem=T.sem["arr%d" % rd],
+                srcs=[view(buf[:, own:own + H])], dsts=[view(buf[:, s:s + H]) for s in spot])], local_sem=T.sem.sent),
+               ["own%d" % rd], ["sent%d" % rd], n_ + "send", fixed=("sent", 2 * lanes * (rd + 1)))
+        op("X", None, [], ["land%d" % rd], n_ + "land", fixed=("arr%d" % rd, 2 * lanes * (N - 1)))
+        if rd == 0:
+            late_constants_c()
+            act(T.c2r[:, 0:C], T.plc[:, 0:S_].indirect(T.oa0[:]), ["plc", "oa0"], ["c2r0"])
+            act(T.c2r[:, C:2 * C], T.c2r[:, 0:C], ["c2r0"], ["c2r"])
+            tt(T.fl[:], ps(3, C), T.h16[:], A.is_gt, ["h16"], ["fla", "flb", "ps3"])
+            qz(T.qe, T.se, 0, 512, T.ee[:], ["ee", "ee1"], ["qe"])
+        scan(T.fs[:], T.fl[:], T.e1[:], A.max, A.mult, ["fla", "flb", "e1"], ["fs"])
+        tt(T.pw[:], T.fs[:, 15::16], T.c0p[:], A.add, ["fs", "c0p"], ["pw"])
+        cp(T.op[:], T.pw[:], ["pw"], ["op"])
+        tt(T.am[:], T.c2r[:].indirect(T.op[:]), T.m16[:], A.mult, ["c2r", "c2r0", "op", "m16"], ["am"])
+        scan(T.aw[:], T.r16[:], T.am[:], A.mult, A.add, ["r16", "am"], ["aw"])
+        tt(T.da[:], T.aw[:, 15::16], T.a0[:], A.subtract, ["aw", "a0"], ["da"])
+        cp(T.oa1[:], T.aw[:, 15::16], ["aw"], ["oa1"])
+        ts(T.db[:], T.da[:], float(S_ - 256), A.is_ge, ["da"], ["db"], -float(S_), A.mult)
+        tt(T.e2[:, 15::16], T.da[:], T.db[:], A.add, ["da", "db"], ["e2"])
+        if last:
+            qz(T.qv, T.sv, 0, 128, T.vt[:], ["vt"], ["qv"])
+        for b in range(4):
+            mx(4 + b, T.qe, T.se, 128 * b, lq, ls, 0, S_, True, True, ["qe", "own%d" % rd, "land%d" % rd])
+        dma("Y", T.hl[:, H * rd:H * rd + H], hh[0:128:16, 0:H], ["hh%d" % rd, "land%d" % rd], ["out_hl%d" % rd])
+        for b in range(4):
+            if b == 0:
+                cp(T.fp[:, 0:S_], ps(4, S_), [], ["fp0", "ps4"])
+            else:
+                act(T.fp[:, S_ * b:S_ * b + S_], ps(4 + b, S_), [], ["fp%d" % b, "ps%d" % (4 + b)])
+        fwin, fkey = (lambda t: T.fp[:, S_ * t:S_ * t + S_]), (lambda t: "fp%d" % t)
+        (a0, a1), (b0, b1) = CH
+        z0 = product(T.z0, T.tg0, 0, C, fwin, fkey, lambda t: T.oa0[:], plane(T.xp, 0, C), ["oa0", xpk], A.mult,
+                     ["z0a", "z0b"], SC[0], n_ + "cz0")
+        z1a = product(T.z1, T.tg1, a0, a1, fwin, fkey, lambda t: T.oa1[:, a0 // 16:a1 // 16], plane(T.xp, a0, a1),
+                      ["oa1", xpk], A.mult, ["z1a"], SC[1], n_ + "cz1a")
+        z1b = product(T.z1, T.tg1, b0, b1, fwin, fkey, lambda t: T.oa1[:, b0 // 16:b1 // 16], plane(T.xp, b0, b1),
+                      ["oa1", xpk], A.mult, ["z1b"], SC[1], n_ + "cz1b")
+        for b in range(4):
+            for d in range(2):
+                act(T.fh[:, 2 * S_ * b + S_ * d:2 * S_ * b + S_ * d + S_], T.fp[:, S_ * b:S_ * b + S_], ["fp%d" % b], ["fh"], 0.5, n_ + "fh")
+
+        def score(a, b, s, bank):
+            keys_ = ["qz1a", "qz1c"] if s == "a" else ["qz1b"]
+            qz(T.qz, T.sz, C + a, C + b, T.z1[:, 4 * a:4 * b], ["z1" + s], keys_)
+            mx(bank, T.qk, T.sk, 0, T.qz, T.sz, C + a, b - a, False, True, keys_)
+
+        def steps(a, b, s, bank):
+            return [
+                lambda: tt(T.fl[:, a:b], ps(bank, b - a), T.h16[:, a:b], A.is_gt, ["h16"], ["fl" + s, "ps%d" % bank]),
+                lambda: scan(T.fs2[:, a:b], T.fl[:, a:b], T.e2[:, a:b], A.max, A.mult, ["fl" + s, "e2"], ["fs" + s]),
+                lambda: tt(T.af[:, a // 16:b // 16], T.fs2[:, a + 15:b:16], T.a0p[:, a // 16:b // 16], A.add, ["fs" + s, "a0p"], ["af" + s]),
+                lambda: cp(T.oa[:, a // 16:b // 16], T.af[:, a // 16:b // 16], ["af" + s], ["oa" + s]),
+            ]
+
+        def mix(a, b, s):
+            return product(T.mm, T.tg0, a, b, lambda t: T.fh[:, 2 * S_ * t:2 * S_ * t + 2 * S_], lambda t: "fh",
+                           lambda t: T.oa[:, a // 16:b // 16], plane(T.xh, a, b), ["oa" + s, "xh"], A.add, ["mm" + s], SM, n_ + "mm" + s)
+
+        def layer(a, b, s, banks):
+            qz(T.qm, T.sm, a, b, T.mm[:, 4 * a:4 * b], ["mm" + s], ["qm" + s])
+            for t in range(4):
+                mx(banks[t], T.qw, T.sw, 128 * t, T.qm, T.sm, a, b - a, True, True, ["qw", "qm" + s])
+
+        def state(a, b, s, banks, t, eng):
+            out = T.xi[:, 4 * a + t:4 * b:4] if last else T.xp[:, C * t + a:C * t + b]
+            wk = ["xi" + s if last else xpk(t), "ps%d" % banks[t]]
+            grp = n_ + "st" + (s if last else str(t))
+            if eng == "V":
+                ts(out, ps(banks[t], b - a), 0.03125, A.mult, [], wk, grp=grp)
+            else:
+                act(out, ps(banks[t], b - a), [], wk, 0.03125, grp)
+
+        def outputs(a, b, s, bank):
+            qz(T.qx, T.sx, a, b, T.xi[:, 4 * a:4 * b], ["xi" + s], ["qx" + s])
+            mx(bank, T.qv, T.sv, 0, T.qx, T.sx, a, b - a, True, True, ["qv", "qx" + s])
+            dma("Y", T.oc[:, 4 * a:4 * b], u8(T.qx[:, a:b]), ["qx" + s], ["out_oc" + s], "out")
+            act(T.ysb[:, a:b], ps(bank, b - a), [], ["ysb" + s, "ps%d" % bank])
+            dma("S", T.y[:, a:b], T.ysb[:, a:b], ["ysb" + s], ["out_y" + s], "out")
+
+        sa_, sb_ = steps(a0, a1, "a", 0), steps(b0, b1, "b", 1)
+        for f in z0:
+            f()
+        z1a[0]()
+        qz(T.qz, T.sz, 0, C, T.z0[:], ["z0a", "z0b"], ["qz0"])
+        mx(0, T.qk, T.sk, 128, T.qz, T.sz, a0, a1 - a0, True, False, ["qz0"])
+        mx(1, T.qk, T.sk, 128, T.qz, T.sz, b0, b1 - b0, True, False, ["qz0"])
+        for f in z1a[1:]:
+            f()
+        z1b[0]()
+        score(a0, a1, "a", 0)
+        for f in z1b[1:]:
+            f()
+        sa_[0]()
+        score(b0, b1, "b", 1)
+        sa_[1]()
+        sa_[2]()
+        sb_[0]()
+        sa_[3]()
+        sb_[1]()
+        ma = mix(a0, a1, "a")
+        ma[0]()
+        sb_[2]()
+        ma[1]()
+        sb_[3]()
+        mb = mix(b0, b1, "b")
+        ma[2]()
+        ma[3]()
+        ba, bb_ = (2, 3, 4, 5), (6, 7, 0, 1)
+        mb[0]()
+        layer(a0, a1, "a", ba)
+        for f in mb[1:]:
+            f()
+        layer(b0, b1, "b", bb_)
+        if last:
+            for t, e in enumerate("SSSV"):
+                state(a0, a1, "a", ba, t, e)
+            state(b0, b1, "b", bb_, 0, "V")
+            outputs(a0, a1, "a", 2)
+            for t in range(1, 4):
+                state(b0, b1, "b", bb_, t, "V")
+            outputs(b0, b1, "b", 3)
+            for k in range(4):
+                dma("Y", T.osc[4 * k:4 * k + 4, :], T.sx[32 * k:32 * k + 4, :], ["qxa", "qxb"], ["out_sc"], "out")
+        else:
+            for t in range(4):
+                state(a0, a1, "a", ba, t, "S")
+                state(b0, b1, "b", bb_, t, "V")
+                if t == 1:
+                    cp(T.xq[:, 0:C], T.xp[:, 0:C], ["xp0"], ["xq0"])
+    op("Y", None, ["out_hl0", "out_hl1", "out_oca", "out_ocb", "out_ya", "out_yb", "out_sc"], [])
+    op("G", None, ["sent%d" % (R - 1)], [])
+    _emit(ops, {"V": V, "S": S, "P": P, "Y": Y, "G": g, "X": None}, T)

@@ -7,16 +7,16 @@ LV = 8
 KB = 64
 BIG = 1e29
 CH = ((0, 256), (256, 384))
-SP, SC, SM = ((0, 0), (0, 0)), (0, 0), 0
+SP, SC, SM = ((0, 2), (2, 3)), (1, 3), 2
 
 BF, F32, I32, U16, Q8, U8 = "bfloat16", "float32", "int32", "uint16", "float8_e4m3fn_x4", "uint8"
 _B = {
     BF: "x0 xp xh xi xq z0 z1 tg0 tg1 mm fh cst:1536 vt bb zb:512 wn:480 gg:2304 dd:1024 o128 n128 t128 d128:128 ee:2048 "
-        "i16 m16 h16 r16 e2 fs2 fl am aw:384 r64 cmp cs:256 eq fp c2r:768",
+        "m16 h16 r16 e2 fs2 fl am aw:384 r64 cmp cs:256 eq fp c2r:768",
     F32: "ysb nc nu e1 fs:384 pf:12 lev one sa va:192 plc tbl:400 zer:4 v1:96 v2 hm hw:48 km kw hh0 hh1:64 "
          "v3 c2a c2b a0 a0p c0p da db pw af:24",
-    I32: "l1 lo hi:48 l2:24 pi:1 pa:4 key kk:384 kp:64",
-    U16: "og:144 o1:192 o1p:48 olb:12 onw:2 nw:32 ork oa0 op oa1 oa:24 or2 oh:4",
+    I32: "l1 lo hi i16:48 l2:24 pi:1 pa:4 key kk:384 kp:64",
+    U16: "og:144 o1:192 o1p om:48 olb:12 onw:2 nw:32 ork oa0 op oa1 oa:24 or2 oh:4",
     Q8: "qz:768 qm qx qk:384 qw qc qe:512 qv:128 qd:256 qq:192 lq0 lq1:272",
     U8: "sz:768 sm sx sk:384 sw sc se:512 sv:128 sd:256 sq:192 ls0 ls1:272",
 }
@@ -186,10 +186,11 @@ def rank_program(g, core, T, topo):
     ts(T.wn[:, 160:320], T.wn[:, 0:160], -1.0, A.add, ["wn0"], ["wn"], -BIG, A.mult, grp="wn")
     ts(T.wn[:, 320:480], T.wn[:, 0:160], -1.0, A.add, ["wn0"], ["wn"], BIG, A.mult, grp="wn")
     gp(lambda: g.affine_select(T.t128[:], T.n128[:], [[-1, 128]], A.is_gt, 0.0, 0, 1), ["n128"], ["t128"])
-    iota(T.i16[:], [[0, 24], [1, 16]], 0, [], ["i16"])
+    gp(lambda: g.affine_select(T.d128[:], T.t128[:], [[-1, 128]], A.not_equal, -512.0, 0, 1), ["t128"], ["d128"])
+    gp(lambda: g.iota(T.i16[:], [[160, 2], [0, 24]], 16, 1), [], ["i16"])
     iota(T.plc[:], [[1, 400]], 0, [], ["plc"])
     iota(T.lev[0:64, :], [[-1, LV], [0, 24]], LV - 1, [], ["lev"])
-    iota(T.lev[64:128, :], [[1, LV], [0, 24]], 0, ["lev", "plc", "i16", "t128", "wn0", "pi"], ["lev2"])
+    iota(T.lev[64:128, :], [[1, LV], [0, 24]], 0, ["lev", "plc", "i16", "d128", "wn0", "pi"], ["lev2"])
 
     ts(T.lo[:], T.l1[:], 15, A.bitwise_and, ["l1"], ["lohi"], grp="lohi")
     ts(T.hi[:], T.l1[:], 4, A.logical_shift_right, ["l1"], ["lohi"], grp="lohi")
@@ -217,21 +218,23 @@ def rank_program(g, core, T, topo):
         dma("Y", T.sw[:], T.ws[:], [], ["qw"], "ldw")
         dma("Y", T.vt[:], T.v[:], [], ["vt"])
 
+    def columns(i):
+        if i == 0:
+            ts(T.pf[:, 8:9], T.pf[:, 2:3], 64.0, A.is_ge, ["pf"], ["pf8"], -64.0, A.mult, grp="pf8")
+            ts(T.pf[:, 4:5], pm, 8.0, A.is_ge, ["pf"], ["pf8"], grp="pf8")
+            cp(T.om[:], T.i16[:], ["i16"], ["om"])
+        elif i == 1:
+            ts(T.pf[:, 7:8], T.pf[:, 2:3], 3.0, A.mult, ["pf", "pf8"], ["pf5"], T.pf[:, 8:9], A.add, grp="pf5")
+            ts(T.pf[:, 5:6], T.pf[:, 4:5], -40.0, A.mult, ["pf8"], ["pf5"], 32.0, A.add, grp="pf5")
+            ts(T.pf[:, 6:7], T.pf[:, 4:5], 16.0, A.mult, ["pf8"], ["pf5"], 8.0, A.add, grp="pf5")
+        elif i == 2:
+            ts(T.pf[:, 3:4], g16, T.pf[:, 7:8], A.add, ["pf", "pf5"], ["pf3"], pm, A.add)
+
     def late_constants_a():
-        ts(T.pf[:, 8:9], T.pf[:, 2:3], 64.0, A.is_ge, ["pf"], ["pf8"], -64.0, A.mult)
-        ts(T.d128[:], T.wn[:, 16:144], -512.0, A.mult, ["wn0"], ["d128"])
-        ts(T.pf[:, 7:8], T.pf[:, 2:3], 3.0, A.mult, ["pf", "pf8"], ["pf7"], T.pf[:, 8:9], A.add)
-        ts(T.m16[:], T.i16[:], pm, A.is_equal, ["i16", "pf"], ["m16"], grp="m16")
-        ts(T.pf[:, 3:4], g16, T.pf[:, 7:8], A.add, ["pf", "pf7"], ["pf3"], pm, A.add, grp="pf3")
-        ts(T.pf[:, 4:5], pm, 8.0, A.is_ge, ["pf"], ["pf3"], grp="pf3")
-        tt(T.cst[:, 1024:1536:4], T.t128[:], T.d128[:], A.add, ["t128", "d128", "cst2"], ["cst3"])
-        ts(T.pf[:, 5:6], T.pf[:, 4:5], -40.0, A.mult, ["pf3"], ["pf5"], 32.0, A.add, grp="pf5")
-        ts(T.pf[:, 6:7], T.pf[:, 4:5], 16.0, A.mult, ["pf3"], ["pf5"], 8.0, A.add, grp="pf5")
-        ts(T.r16[:], T.i16[:], 0.0, A.is_gt, ["i16"], ["r16"], grp="m16")
         qz(T.qk, T.sk, 256, 384, T.cst[:, 1024:1536], ["cst3", "cst2"], ["qk2"])
         ts(T.olb[:, 0:12:3], T.zer[:], T.pf[:, 3:4], A.add, ["pf3", "zer"], ["olb"], grp="olb")
-        ts(T.olb[:, 1:12:3], T.zer[:], T.pf[:, 3:4], A.add, ["pf5", "zer"], ["olb"], T.pf[:, 5:6], A.add, grp="olb")
-        ts(T.olb[:, 2:12:3], T.zer[:], T.pf[:, 3:4], A.add, ["pf5", "zer"], ["olb"], T.pf[:, 6:7], A.add, grp="olb")
+        ts(T.olb[:, 1:12:3], T.zer[:], T.pf[:, 3:4], A.add, ["pf3", "pf5", "zer"], ["olb"], T.pf[:, 5:6], A.add, grp="olb")
+        ts(T.olb[:, 2:12:3], T.zer[:], T.pf[:, 3:4], A.add, ["pf3", "pf5", "zer"], ["olb"], T.pf[:, 6:7], A.add, grp="olb")
         ts(T.onw[:, 0:1], T.pf[:, 3:4], 0.0, A.add, ["pf3"], ["onw"], grp="olb")
         ts(T.onw[:, 1:2], T.pf[:, 3:4], 32.0, A.add, ["pf3"], ["onw"], grp="olb")
 
@@ -278,11 +281,11 @@ def rank_program(g, core, T, topo):
             turns(0)
             qz(T.qk, T.sk, 0, 256, T.cst[:, 0:1024], ["cst0", "cst1"], ["qk"])
             turns(1)
-            src, sk = (lambda t: T.x0[:, t::4]), (lambda t: "x0")
+            src, sk, nq = (lambda t: T.x0[:, t::4]), (lambda t: "x0"), 4
             cp(T.xq[:, 0:C], src(0), ["x0"], ["xq0"])
         else:
-            src, sk = plane(T.xp, 0, C), xpk
-        for t in range(1, 4):
+            src, sk, nq = plane(T.xp, 0, C), xpk, 4 - min(SP[rd])
+        for t in range(1, nq):
             act(T.xq[:, C * t:C * t + C], src(t), [sk(t)], ["xq%d" % t])
         if rd == 0:
             turns(2)
@@ -294,13 +297,18 @@ def rank_program(g, core, T, topo):
                 win, off = (lambda t: T.x0[:]), (lambda t, k=k: T.o1[:, 48 * t + 24 * k:48 * t + 24 * k + 24])
             else:
                 win, off = plane(T.xp, 0, C), (lambda t, k=k: T.o1p[:, 24 * k:24 * k + 24])
-            w.append(product(z, tg, 0, C, win, sk, off, plane(T.xq, 0, C),
-                             ["o1" if rd == 0 else "o1p", lambda t: "xq%d" % t], A.mult, zk, SP[rd][k], n_ + "pz%d" % k))
-        for f in w[0]:
+            w.append(product(z, tg, 0, C, win, sk, off, lambda t, nq=nq: (T.xq if t < nq else T.xp)[:, C * t:C * t + C],
+                             ["o1" if rd == 0 else "o1p", lambda t, nq=nq: ("xq%d" if t < nq else "xp%d") % t],
+                             A.mult, zk, SP[rd][k], n_ + "pz%d" % k))
+        for i, f in enumerate(w[0]):
+            if i == 2 and SP[rd][0] >= 2:
+                w[1][0]()
             f()
-        w[1][0]()
+            if rd == 0:
+                columns(i)
+        w[1][1 if SP[rd][0] >= 2 else 0]()
         qz(T.qz, T.sz, 0, C, T.z0[:], ["z0a", "z0b"], ["qz0"])
-        for f in w[1][1:]:
+        for f in w[1][2 if SP[rd][0] >= 2 else 1:]:
             f()
         for t in range(3):
             mx(t, T.qz, T.sz, 128 * t, T.qk, T.sk, 128, 128, True, False, ["qz0", "qk"])
@@ -311,9 +319,14 @@ def rank_program(g, core, T, topo):
             mx(t, T.qz, T.sz, C + 128 * t, T.qk, T.sk, 0, 128, False, True, q1[t] + ["qk"])
         mx(3, T.qk, T.sk, 0, T.qz, T.sz, C, C, False, True, ["qz1a", "qz1b", "qz1c", "qk"])
         if rd == 0:
-            act(T.xp[:], T.xq[:], ["xq0", "xq1", "xq2", "xq3"], xps)
+            act(T.cst[:, 1024:1536:4], T.d128[:], ["d128", "cst2"], ["cst3"])
             act(T.tbl[:], T.plc[:], ["plc"], ["tbl"], -512.0, None, float(C * 512))
-            act(T.e1[:], T.zb[:, 0:C], ["zb"], ["e1"], 1.0, None, 1.0)
+            act(T.m16[:], T.wn[:].indirect(T.om[:, 0:24]), ["wn", "wn0", "om"], ["m16"])
+            act(T.r16[:], T.zb[:, 0:C], ["zb"], ["r16"], 1.0, None, 1.0)
+            act(T.h16[:], T.wn[:].indirect(T.om[:, 24:48]), ["wn", "wn0", "om"], ["h16"])
+            act(T.r16[:, 0::16], T.zb[:, 0:24], ["zb"], ["r16"])
+            for b in range(4):
+                act(T.ee[:, 512 * b:512 * b + 512], T.zb[:], ["zb"], ["ee"], grp="ee")
             late_constants_a()
             for a in range(4):
                 qz(T.qc, T.sc, 128 * a, 128 * a + 128, T.tt[:, a, 256:768], ["tt"], ["qc"], "qc")
@@ -327,7 +340,6 @@ def rank_program(g, core, T, topo):
             mx(7, T.qd, T.sd, 128 * k, T.qc, T.sc, 256 + 64 * k, 192, k == 0, k == 1, ["qd%d" % k, "qc"])
             mx(4, T.qd, T.sd, 128 * k, T.qc, T.sc, 64 * k, 192, k == 0, k == 1, ["qd%d" % k, "qc"])
         if rd == 0:
-            ts(T.h16[:], T.i16[:], pm, A.not_equal, ["i16", "pf"], ["h16"], BIG, A.mult)
             ms(T.r64[:], 1.0, ["r64"])
         else:
             tt(T.fl[:], ps(3, C), T.h16[:], A.is_gt, ["h16"], ["fla", "flb", "ps3"])
@@ -337,12 +349,11 @@ def rank_program(g, core, T, topo):
         act(T.nu[:, 0:192], ps(4, 192), [], ["nu", "ps4"], grp=n_ + "nu")
         if rd == 0:
             ms(T.r64[:, 0::64], 0.0, ["r64"])
-            act(T.e2[:], T.zb[:, 0:C], ["zb"], ["e2"], 1.0, None, 1.0)
-            act(T.xh[:], T.xp[:], xps, ["xh"], 0.5)
-            for b in range(4):
-                act(T.ee[:, 512 * b:512 * b + 512], T.zb[:], ["zb"], ["ee"], grp="ee")
+            act(T.xp[:], T.xq[:], ["xq0", "xq1", "xq2", "xq3"], xps)
             for b in range(4):
                 act(T.ee[:, 512 * b + b:512 * b + 512:4], T.wn[:, 16:144], ["wn0", "ee"], ["ee1"], grp="ee1")
+            act(T.e1[:], T.zb[:, 0:C], ["zb"], ["e1"], 1.0, None, 1.0)
+            act(T.e2[:], T.zb[:, 0:C], ["zb"], ["e2"], 1.0, None, 1.0)
         tt(T.eq[:, 0::4], T.nc[:].indirect(T.olb[:]), T.lev[:], A.is_equal, ["nc", "nc2", "olb", "lev", "lev2", "eq0"], ["eq"])
         qz(T.qq, T.sq, 0, 192, T.eq[:], ["eq", "eq0"], ["qq"])
         mx(5, T.qk, T.sk, 0, T.qq, T.sq, 0, 192, True, True, ["qq", "qk"])
@@ -377,7 +388,7 @@ def rank_program(g, core, T, topo):
         scan(T.hw[:], T.r16[:, 0:H], T.hm[:], A.mult, A.add, ["r16", "hm"], ["hw"])
         cp(T.oh[:, 0:3], T.hw[:, 15::16], ["hw"], ["oh"])
         for t in range(4):
-            cp(T.bb[:, t:4 * H:4], T.xp[:, C * t:C * t + C].indirect(T.oh[:, 0:3]), [xpk(t), "oh", "bb0"], ["bb"], n_ + "bb")
+            (cp if t < 2 else act)(T.bb[:, t:4 * H:4], T.xp[:, C * t:C * t + C].indirect(T.oh[:, 0:3]), [xpk(t), "oh", "bb0"], ["bb"], grp=n_ + "bb")
         lq, ls = T["lq%d" % rd], T["ls%d" % rd]
         qz(lq, ls, own, own + 128, T.bb[:], ["bb", "bb0"], ["own%d" % rd])
         for buf, view in ((lq, u8), (ls, lambda ap: ap)):
@@ -390,6 +401,7 @@ def rank_program(g, core, T, topo):
             late_constants_c()
             act(T.c2r[:, 0:C], T.plc[:, 0:S_].indirect(T.oa0[:]), ["plc", "oa0"], ["c2r0"])
             act(T.c2r[:, C:2 * C], T.c2r[:, 0:C], ["c2r0"], ["c2r"])
+            act(T.xh[:], T.xp[:], xps, ["xh"], 0.5)
             tt(T.fl[:], ps(3, C), T.h16[:], A.is_gt, ["h16"], ["fla", "flb", "ps3"])
             qz(T.qe, T.se, 0, 512, T.ee[:], ["ee", "ee1"], ["qe"])
         scan(T.fs[:], T.fl[:], T.e1[:], A.max, A.mult, ["fla", "flb", "e1"], ["fs"])

@@ -6,17 +6,19 @@ S_ = N * H
 LV = 8
 KB = 64
 BIG = 1e29
+KS, KL = 256.0, 2048.0
 CH = ((0, 256), (256, 384))
-SP, SC, SM = ((0, 2), (2, 3)), (1, 3), 2
+SP, SC, SM = ((0, 3), (2, 3)), (2, 3), 2
+ORDER = ("iajTbUkcVsdqefgh", "abecdfqgh")
 
 BF, F32, I32, U16, Q8, U8 = "bfloat16", "float32", "int32", "uint16", "float8_e4m3fn_x4", "uint8"
 _B = {
-    BF: "x0 xp xh xi xq z0 z1 tg0 tg1 mm fh cst:1536 vt bb zb:512 wn:480 gg:2304 dd:1024 o128 n128 t128 d128:128 ee:2048 "
-        "m16 h16 r16 e2 fs2 fl am aw:384 r64 cmp cs:256 eq fp c2r:768",
-    F32: "ysb nc nu e1 fs:384 pf:12 lev one sa va:192 plc tbl:400 zer:4 v1:96 v2 hm hw:48 km kw hh0 hh1:64 "
-         "v3 c2a c2b a0 a0p c0p da db pw af:24",
-    I32: "l1 lo hi i16:48 l2:24 pi:1 pa:4 key kk:384 kp:64",
-    U16: "og:144 o1:192 o1p om:48 olb:12 onw:2 nw:32 ork oa0 op oa1 oa:24 or2 oh:4",
+    BF: "x0 x1 xp xh x2 xi xq z0 z1 tg0 tg1 mm fp cst:1536 vt bb zb:512 wn:480 gg:2304 dd:1024 o128 n128 t128 d128 cw:128 ee:2048 "
+        "c16 h16 c2r e1 e2 fl fs fs2:384 r64 cmp cs:256 eq ar aw:768 c64:64",
+    F32: "ysb nc nu key kk:384 pf:12 lev one sa va:192 plc tbl:400 v1:96 v2 hw:48 kw hh0 hh1:64 "
+         "v3 c2a c2b a0 a0p b0 b1 nd t1 a1 da db af:24",
+    I32: "l1 lo hi i16:48 l2:24 pi:1 pa:4 ki:64",
+    U16: "og:144 o1:192 o1p om:48 olb:12 onw:2 nw:32 ork oa0 oa1 oa:24 or2 oh:4",
     Q8: "qz:768 qm qx qk:384 qw qc qe:512 qv:128 qd:256 qq:192 lq0 lq1:272",
     U8: "sz:768 sm sx sk:384 sw sc se:512 sv:128 sd:256 sq:192 ls0 ls1:272",
 }
@@ -156,55 +158,55 @@ def rank_program(g, core, T, topo):
 
     dma("Y", T.l1[:], T.c1[:], [], ["l1"])
     dma("Y", T.x0[:], T.x[:], [], ["x0"])
+    dma("Y", T.x1[:], T.x[:], [], ["x1"])
     dma("Y", T.l2[:], T.c2[:], [], ["l2"])
 
     gp(lambda: g.iota(T.pi[:], [[0, 1]], 0, 1), [], ["pi"])
     ms(T.o128[:], 1.0, ["o128"])
     ms(T.wn[:, 0:160], 1.0, ["wn0"])
     ms(T.zb[:], 0.0, ["zb"])
+    gp(lambda: g.affine_select(T.wn[:, 0:160], T.wn[:, 0:160], [[-1, 160]], A.is_equal, 0.0, 16, 1), ["wn0"], ["wn0"])
     gp(lambda: g.affine_select(T.o128[:], T.o128[:], [[-16, 8], [0, 16]], A.is_ge, 0.0, 0, 1), ["o128"], ["o128"])
     gp(lambda: g.affine_select(T.o128[:], T.o128[:], [[16, 8], [0, 16]], A.is_ge, 0.0, 15, -1), ["o128"], ["o128"])
-    gp(lambda: g.affine_select(T.wn[:, 0:160], T.wn[:, 0:160], [[-1, 160]], A.is_equal, 0.0, 16, 1), ["wn0"], ["wn0"])
     ts(T.pa[:, 0:1], T.pi[:], 128 - 16, A.bitwise_and, ["pi"], ["pa"], grp="pa")
     ts(T.pa[:, 1:2], T.pi[:], 15, A.bitwise_and, ["pi"], ["pa"], grp="pa")
     ts(T.pa[:, 2:3], T.pi[:], 128 - 32, A.bitwise_and, ["pi"], ["pa"], grp="pa")
-    for a in range(4):
-        ms(T.gt[:, a, 3::4], 0.0, ["gt3"], "fill")
-    ms(T.dd[:, 3::4], 0.0, ["dd3"], "fill")
-    ms(T.zer[:], 0.0, ["zer"], "fill")
+    ms(T.r64[:], 1.0, ["r64"])
     cp(T.pf[:, 0:3], T.pa[:, 0:3], ["pa"], ["pf"])
     g16, pm = T.pf[:, 0:1], T.pf[:, 1:2]
-    act(T.eq[:, 0:512], T.zb[:], ["zb"], ["eq0"], grp="fs")
-    act(T.eq[:, 512:768], T.zb[:, 0:256], ["zb"], ["eq0"], grp="fs")
-    act(T.bb[:], T.zb[:], ["zb"], ["bb0"], grp="fs")
-    act(T.cst[:, 1024:1536], T.zb[:], ["zb"], ["cst2"], grp="fs")
-    act(T.one[:], T.zb[:, 0:192], ["zb"], ["one"], 1.0, "fs", 1.0)
-    ts(T.n128[:], T.o128[:], -1.0, A.mult, ["o128"], ["n128"])
-    for t in range(4):
-        cp(T.cst[:, t:512:4], T.o128[:], ["o128"], ["cst0"], "cst0")
-    ts(T.cst[:, 512:1024], T.cst[:, 0:512], -1.0, A.mult, ["cst0"], ["cst1"])
-    ts(T.wn[:, 160:320], T.wn[:, 0:160], -1.0, A.add, ["wn0"], ["wn"], -BIG, A.mult, grp="wn")
-    ts(T.wn[:, 320:480], T.wn[:, 0:160], -1.0, A.add, ["wn0"], ["wn"], BIG, A.mult, grp="wn")
+    act(T.wn[:, 160:320], T.wn[:, 0:160], ["wn0"], ["wn"], -BIG, "wn", BIG)
+    act(T.wn[:, 320:480], T.wn[:, 0:160], ["wn0"], ["wn"], BIG, "wn", -BIG)
+    act(T.dd[:, 3::4], T.zb[:, 0:256], ["zb"], ["dd3"])
+    act(T.n128[:], T.o128[:], ["o128"], ["n128"], -1.0)
+    for a in range(4):
+        ms(T.gt[:, a, 3::4], 0.0, ["gt3"], "fill")
     gp(lambda: g.affine_select(T.t128[:], T.n128[:], [[-1, 128]], A.is_gt, 0.0, 0, 1), ["n128"], ["t128"])
+    gp(lambda: g.iota(T.i16[:], [[176, 2], [0, 24]], 0, 1), [], ["i16"])
     gp(lambda: g.affine_select(T.d128[:], T.t128[:], [[-1, 128]], A.not_equal, -512.0, 0, 1), ["t128"], ["d128"])
-    gp(lambda: g.iota(T.i16[:], [[160, 2], [0, 24]], 16, 1), [], ["i16"])
     iota(T.plc[:], [[1, 400]], 0, [], ["plc"])
     iota(T.lev[0:64, :], [[-1, LV], [0, 24]], LV - 1, [], ["lev"])
     iota(T.lev[64:128, :], [[1, LV], [0, 24]], 0, ["lev", "plc", "i16", "d128", "wn0", "pi"], ["lev2"])
+    gp(lambda: g.affine_select(T.cw[:], T.zb[:, 0:128], [[-1, 128]], A.not_equal, 4.0 * KS, 0, 1), ["zb", "lev2"], ["cw0"])
+    gp(lambda: g.affine_select(T.cw[:], T.cw[:], [[-1, 128]], A.not_equal, -KS, 1, 1), ["cw0"], ["cw"])
+    for b in range(4):
+        gp(lambda b=b: g.affine_select(T.ee[:, 512 * b:512 * b + 512], T.zb[:], [[-4, 128], [-1, 4]], A.not_equal, 1.0, b, 4),
+           ["zb", "cw"], ["ee%d" % b])
 
     ts(T.lo[:], T.l1[:], 15, A.bitwise_and, ["l1"], ["lohi"], grp="lohi")
     ts(T.hi[:], T.l1[:], 4, A.logical_shift_right, ["l1"], ["lohi"], grp="lohi")
-    ts(T.o1[:, 0:48], T.l1[:], 4.0, A.mult, ["l1"], ["o1"], grp="o1")
+    ms(T.r64[:, 0::64], 0.0, ["r64"])
     for y, (src, k, c) in enumerate(((T.lo, 0, 336), (T.lo, 1, 176), (T.hi, 0, 16), (T.hi, 0, 0), (T.hi, 1, 16), (T.hi, 1, 0))):
         ts(T.vals[:, y], src[:, 24 * k:24 * k + 24], g16, A.add, ["lohi", "pf"], ["vals"], float(c), A.add, grp="vals")
-    ts(T.o1[:, 48:96], T.l1[:], 4.0, A.mult, ["l1"], ["o1"], 1.0, A.add, grp="o1")
-    for t in (1, 2, 0):
+    ts(T.o1[:, 0:48], T.l1[:], 4.0, A.mult, ["l1"], ["o1"], grp="o1")
+    for t in range(3):
         cp(T.og[:, 48 * t:48 * t + 48], T.vals[:, :, t, :], ["vals"], ["og%d" % t])
-    for t in range(2, 4):
+    for t in range(1, 4):
         ts(T.o1[:, 48 * t:48 * t + 48], T.l1[:], 4.0, A.mult, ["l1"], ["o1"], float(t), A.add, grp="o1")
-    for t in (1, 2):
+    for t in range(4):
+        act(T.cst[:, t:512:4], T.o128[:], ["o128"], ["cst0"], None, "cst0")
+    ts(T.cst[:, 512:1024], T.cst[:, 0:512], -1.0, A.mult, ["cst0"], ["cst1"])
+    for t in range(3):
         act(T.gg[:, 768 * t:768 * t + 768], T.wn[:].indirect(T.og[:, 48 * t:48 * t + 48]), ["wn", "wn0", "og%d" % t], ["gg%d" % t])
-    cp(T.gg[:, 0:768], T.wn[:].indirect(T.og[:, 0:48]), ["wn", "wn0", "og0"], ["gg0"])
 
     def turns(t):
         for a in range(4):
@@ -222,31 +224,28 @@ def rank_program(g, core, T, topo):
         if i == 0:
             ts(T.pf[:, 8:9], T.pf[:, 2:3], 64.0, A.is_ge, ["pf"], ["pf8"], -64.0, A.mult, grp="pf8")
             ts(T.pf[:, 4:5], pm, 8.0, A.is_ge, ["pf"], ["pf8"], grp="pf8")
-            cp(T.om[:], T.i16[:], ["i16"], ["om"])
+            ts(T.pf[:, 9:10], pm, 15.0, A.not_equal, ["pf"], ["pf9a"], KS, A.mult, grp="pf8")
         elif i == 1:
             ts(T.pf[:, 7:8], T.pf[:, 2:3], 3.0, A.mult, ["pf", "pf8"], ["pf5"], T.pf[:, 8:9], A.add, grp="pf5")
             ts(T.pf[:, 5:6], T.pf[:, 4:5], -40.0, A.mult, ["pf8"], ["pf5"], 32.0, A.add, grp="pf5")
             ts(T.pf[:, 6:7], T.pf[:, 4:5], 16.0, A.mult, ["pf8"], ["pf5"], 8.0, A.add, grp="pf5")
         elif i == 2:
             ts(T.pf[:, 3:4], g16, T.pf[:, 7:8], A.add, ["pf", "pf5"], ["pf3"], pm, A.add)
+            cp(T.om[:], T.i16[:], ["i16"], ["om"])
 
     def late_constants_a():
+        zer = T.zb[:, 0:4]
         qz(T.qk, T.sk, 256, 384, T.cst[:, 1024:1536], ["cst3", "cst2"], ["qk2"])
-        ts(T.olb[:, 0:12:3], T.zer[:], T.pf[:, 3:4], A.add, ["pf3", "zer"], ["olb"], grp="olb")
-        ts(T.olb[:, 1:12:3], T.zer[:], T.pf[:, 3:4], A.add, ["pf3", "pf5", "zer"], ["olb"], T.pf[:, 5:6], A.add, grp="olb")
-        ts(T.olb[:, 2:12:3], T.zer[:], T.pf[:, 3:4], A.add, ["pf3", "pf5", "zer"], ["olb"], T.pf[:, 6:7], A.add, grp="olb")
+        ts(T.olb[:, 0:12:3], zer, T.pf[:, 3:4], A.add, ["pf3", "zb"], ["olb"], grp="olb")
+        ts(T.olb[:, 1:12:3], zer, T.pf[:, 3:4], A.add, ["pf3", "pf5", "zb"], ["olb"], T.pf[:, 5:6], A.add, grp="olb")
+        ts(T.olb[:, 2:12:3], zer, T.pf[:, 3:4], A.add, ["pf3", "pf5", "zb"], ["olb"], T.pf[:, 6:7], A.add, grp="olb")
         ts(T.onw[:, 0:1], T.pf[:, 3:4], 0.0, A.add, ["pf3"], ["onw"], grp="olb")
         ts(T.onw[:, 1:2], T.pf[:, 3:4], 32.0, A.add, ["pf3"], ["onw"], grp="olb")
 
     def late_constants_c():
         ts(T.c2a[:], T.l2[:], float(S_ - H * (me + 1)), A.add, ["l2"], ["c2a"])
-        ts(T.c0p[:], T.l1[:, 0:24], float(C), A.add, ["l1"], ["c0p"])
-        ts(T.c2b[:], T.c2a[:], float(S_), A.is_ge, ["c2a"], ["c2b"], -float(S_), A.mult)
         cp(T.o1p[:], T.l1[:], ["l1"], ["o1p"])
-        tt(T.a0[:], T.c2a[:], T.c2b[:], A.add, ["c2a", "c2b"], ["a0"])
-        tt(T.e1[:, 15::16], T.l1[:, 24:48], T.c0p[:], A.subtract, ["l1", "c0p"], ["e1"])
-        cp(T.oa0[:], T.a0[:], ["a0"], ["oa0"], "oa0")
-        ts(T.a0p[:], T.a0[:], float(S_), A.add, ["a0"], ["a0p"], grp="oa0")
+        ts(T.c2b[:], T.c2a[:], float(S_), A.is_ge, ["c2a"], ["c2b"], -float(S_), A.mult)
 
     peers = [c for c in T.cores if c != core]
     mask = topo.mask(core, peers[0])
@@ -278,38 +277,29 @@ def rank_program(g, core, T, topo):
         n_ = "r%d" % rd
         last = rd == R - 1
         if rd == 0:
-            turns(0)
             qz(T.qk, T.sk, 0, 256, T.cst[:, 0:1024], ["cst0", "cst1"], ["qk"])
-            turns(1)
-            src, sk, nq = (lambda t: T.x0[:, t::4]), (lambda t: "x0"), 4
-            cp(T.xq[:, 0:C], src(0), ["x0"], ["xq0"])
+            sk, nq = (lambda t: "x0"), 0
         else:
-            src, sk, nq = plane(T.xp, 0, C), xpk, 4 - min(SP[rd])
+            sk, nq = xpk, 4 - min(SP[rd])
         for t in range(1, nq):
-            act(T.xq[:, C * t:C * t + C], src(t), [sk(t)], ["xq%d" % t])
-        if rd == 0:
-            turns(2)
-            shuffles()
+            act(T.xq[:, C * t:C * t + C], T.xp[:, C * t:C * t + C], [sk(t)], ["xq%d" % t])
         w = []
         for k, (z, tg) in enumerate(((T.z0, T.tg0), (T.z1, T.tg1))):
             zk = ["z%da" % k, "z%db" % k]
             if rd == 0:
                 win, off = (lambda t: T.x0[:]), (lambda t, k=k: T.o1[:, 48 * t + 24 * k:48 * t + 24 * k + 24])
+                oth, oks = (lambda t: T.x1[:, t::4]), ["o1", "x1"]
             else:
                 win, off = plane(T.xp, 0, C), (lambda t, k=k: T.o1p[:, 24 * k:24 * k + 24])
-            w.append(product(z, tg, 0, C, win, sk, off, lambda t, nq=nq: (T.xq if t < nq else T.xp)[:, C * t:C * t + C],
-                             ["o1" if rd == 0 else "o1p", lambda t, nq=nq: ("xq%d" if t < nq else "xp%d") % t],
-                             A.mult, zk, SP[rd][k], n_ + "pz%d" % k))
-        for i, f in enumerate(w[0]):
-            if i == 2 and SP[rd][0] >= 2:
-                w[1][0]()
-            f()
-            if rd == 0:
-                columns(i)
-        w[1][1 if SP[rd][0] >= 2 else 0]()
-        qz(T.qz, T.sz, 0, C, T.z0[:], ["z0a", "z0b"], ["qz0"])
-        for f in w[1][2 if SP[rd][0] >= 2 else 1:]:
-            f()
+                oth = lambda t, nq=nq: (T.xq if t < nq else T.xp)[:, C * t:C * t + C]
+                oks = ["o1p", lambda t, nq=nq: ("xq%d" if t < nq else "xp%d") % t]
+            w.append(product(z, tg, 0, C, win, sk, off, oth, oks, A.mult, zk, SP[rd][k], n_ + "pz%d" % k))
+        step = dict(zip("abcdefgh", w[0] + w[1]))
+        step.update(q=lambda: qz(T.qz, T.sz, 0, C, T.z0[:], ["z0a", "z0b"], ["qz0"]), s=shuffles,
+                    T=lambda: turns(0), U=lambda: turns(1), V=lambda: turns(2),
+                    i=lambda: columns(0), j=lambda: columns(1), k=lambda: columns(2))
+        for c in ORDER[rd]:
+            step[c]()
         for t in range(3):
             mx(t, T.qz, T.sz, 128 * t, T.qk, T.sk, 128, 128, True, False, ["qz0", "qk"])
         mx(3, T.qk, T.sk, 128, T.qz, T.sz, 0, C, True, False, ["qz0", "qk"])
@@ -319,28 +309,34 @@ def rank_program(g, core, T, topo):
             mx(t, T.qz, T.sz, C + 128 * t, T.qk, T.sk, 0, 128, False, True, q1[t] + ["qk"])
         mx(3, T.qk, T.sk, 0, T.qz, T.sz, C, C, False, True, ["qz1a", "qz1b", "qz1c", "qk"])
         if rd == 0:
+            act(T.cst[:, 1024:1536], T.zb[:], ["zb"], ["cst2"])
+            act(T.eq[:, 0:512], T.zb[:], ["zb"], ["eq0"], grp="fs")
             act(T.cst[:, 1024:1536:4], T.d128[:], ["d128", "cst2"], ["cst3"])
+            act(T.eq[:, 512:768], T.zb[:, 0:256], ["zb"], ["eq0"], grp="fs")
+            act(T.one[:], T.zb[:, 0:192], ["zb"], ["one"], 1.0, "fs", 1.0)
             act(T.tbl[:], T.plc[:], ["plc"], ["tbl"], -512.0, None, float(C * 512))
-            act(T.m16[:], T.wn[:].indirect(T.om[:, 0:24]), ["wn", "wn0", "om"], ["m16"])
-            act(T.r16[:], T.zb[:, 0:C], ["zb"], ["r16"], 1.0, None, 1.0)
+            act(T.c16[:], T.cw[:].indirect(T.om[:, 0:24]), ["cw", "om"], ["c16"])
             act(T.h16[:], T.wn[:].indirect(T.om[:, 24:48]), ["wn", "wn0", "om"], ["h16"])
-            act(T.r16[:, 0::16], T.zb[:, 0:24], ["zb"], ["r16"])
-            for b in range(4):
-                act(T.ee[:, 512 * b:512 * b + 512], T.zb[:], ["zb"], ["ee"], grp="ee")
-            late_constants_a()
+            act(T.bb[:], T.zb[:], ["zb"], ["bb0"])
+            act(T.c64[:], T.c16[:, 0:KB], ["c16"], ["c64"], KL)
+            act(T.pf[:, 10:11], T.pf[:, 9:10], ["pf9a"], ["pf9"], KL, "pf9")
+            act(T.pf[:, 11:12], T.pf[:, 9:10], ["pf9a"], ["pf9"], -KL, "pf9")
             for a in range(4):
                 qz(T.qc, T.sc, 128 * a, 128 * a + 128, T.tt[:, a, 256:768], ["tt"], ["qc"], "qc")
         else:
-            act(T.xh[:], T.xp[:], xps, ["xh"], 0.5)
+            act(T.x2[:], T.xp[:], xps, ["x2"], 2.0)
         for k, alu in enumerate((A.is_le, A.is_gt)):
             for t in range(3):
                 tt(T.dd[:, 512 * k + t:512 * k + 512:4], ps(t, 128), T.tt[:, :, 128 * k + t:128 * k + 128:4], alu,
                    ["tt"], ["dd%d" % k, "ps%d" % t], n_ + "dd%d" % k)
+            if rd == 0 and k == 0:
+                late_constants_c()
             qz(T.qd, T.sd, 128 * k, 128 * k + 128, T.dd[:, 512 * k:512 * k + 512], ["dd%d" % k, "dd3"], ["qd%d" % k])
             mx(7, T.qd, T.sd, 128 * k, T.qc, T.sc, 256 + 64 * k, 192, k == 0, k == 1, ["qd%d" % k, "qc"])
             mx(4, T.qd, T.sd, 128 * k, T.qc, T.sc, 64 * k, 192, k == 0, k == 1, ["qd%d" % k, "qc"])
         if rd == 0:
-            ms(T.r64[:], 1.0, ["r64"])
+            late_constants_a()
+            tt(T.a0[:], T.c2a[:], T.c2b[:], A.add, ["c2a", "c2b"], ["a0"])
         else:
             tt(T.fl[:], ps(3, C), T.h16[:], A.is_gt, ["h16"], ["fla", "flb", "ps3"])
         ts(T.nc[:, 0:192], ps(4, 192), float(LV - 1), A.min, [], ["nc", "ps4"])
@@ -348,12 +344,17 @@ def rank_program(g, core, T, topo):
         act(T.nu[:, 192:384], ps(7, 192), [], ["nu", "ps7"], grp=n_ + "nu")
         act(T.nu[:, 0:192], ps(4, 192), [], ["nu", "ps4"], grp=n_ + "nu")
         if rd == 0:
-            ms(T.r64[:, 0::64], 0.0, ["r64"])
-            act(T.xp[:], T.xq[:], ["xq0", "xq1", "xq2", "xq3"], xps)
-            for b in range(4):
-                act(T.ee[:, 512 * b + b:512 * b + 512:4], T.wn[:, 16:144], ["wn0", "ee"], ["ee1"], grp="ee1")
+            cp(T.oa0[:], T.a0[:], ["a0"], ["oa0"])
+            act(T.c2r[:], T.plc[:, 0:S_].indirect(T.oa0[:]), ["plc", "oa0"], ["c2r"])
+            for t in range(4):
+                act(T.x2[:, C * t:C * t + C], T.x0[:, t::4], ["x0"], ["x2"], 2.0, "x2")
+            act(T.ar[:], T.c2r[:].indirect(T.o1p[:]), ["c2r", "o1p"], ["ar"])
             act(T.e1[:], T.zb[:, 0:C], ["zb"], ["e1"], 1.0, None, 1.0)
             act(T.e2[:], T.zb[:, 0:C], ["zb"], ["e2"], 1.0, None, 1.0)
+            act(T.e1[:, 15::16], T.zb[:, 0:24], ["zb"], ["e1"], 1.0, None, -1.0)
+            act(T.a0p[:], T.a0[:], ["a0"], ["a0p"], 1.0, None, float(S_))
+        else:
+            act(T.xh[:], T.xp[:], xps, ["xh"], 0.5)
         tt(T.eq[:, 0::4], T.nc[:].indirect(T.olb[:]), T.lev[:], A.is_equal, ["nc", "nc2", "olb", "lev", "lev2", "eq0"], ["eq"])
         qz(T.qq, T.sq, 0, 192, T.eq[:], ["eq", "eq0"], ["qq"])
         mx(5, T.qk, T.sk, 0, T.qq, T.sq, 0, 192, True, True, ["qq", "qk"])
@@ -376,19 +377,23 @@ def rank_program(g, core, T, topo):
         ts(T.ork[:], T.v3[:], 511.0, A.add, ["v3"], ["ork"])
         cp(T.kk[:].indirect(T.ork[:]), T.key[:], ["ork", "key"], ["kk"])
         hh = T["hh%d" % rd]
-        tt(T.km[:], T.kk[:, 0:KB], T.m16[:, 0:KB], A.mult, ["kk", "m16"], ["km"])
-        ts(T.kp[:], T.kk[:, 0:KB], 511, A.bitwise_and, ["kk"], ["kp"])
-        scan(T.kw[:], T.r16[:, 0:KB], T.km[:], A.mult, A.add, ["r16", "km"], ["kw"])
+        scan(T.kw[:], T.c64[:], T.kk[:, 0:KB], A.add, A.min, ["c64", "kk"], ["kw"])
+        cp(T.ki[:], T.kk[:, 0:KB], ["kk"], ["ki"])
         for m in range(4):
-            ts(T.cmp[:, KB * m:KB * m + KB], T.kk[:, 0:KB], T.kw[:, 16 * m + 15:16 * m + 16], A.is_lt, ["kk", "kw"], ["cmp"], grp=n_ + "cmp")
+            ts(T.cmp[:, KB * m:KB * m + KB], T.kk[:, 0:KB], T.pf[:, 11:12], A.add, ["kk", "kw", "pf9"], ["cmp"],
+               T.kw[:, 16 * m + 15:16 * m + 16], A.is_lt, grp=n_ + "cmp")
+        ts(T.ki[:], T.ki[:], 511, A.bitwise_and, ["ki"], ["ki"])
         scan(T.cs[:], T.r64[:], T.cmp[:], A.mult, A.add, ["r64", "cmp"], ["cs"])
         cp(T.or2[:], T.cs[:, KB - 1::KB], ["cs"], ["or2"])
-        cp(hh[:].indirect(T.or2[:]), T.kp[:], ["or2", "kp"], ["hh%d" % rd])
-        tt(T.hm[:], hh[:, 0:H], T.m16[:, 0:H], A.mult, ["hh%d" % rd, "m16"], ["hm"])
-        scan(T.hw[:], T.r16[:, 0:H], T.hm[:], A.mult, A.add, ["r16", "hm"], ["hw"])
-        cp(T.oh[:, 0:3], T.hw[:, 15::16], ["hw"], ["oh"])
+        cp(hh[:].indirect(T.or2[:]), T.ki[:], ["or2", "ki"], ["hh%d" % rd])
+        scan(T.hw[:], T.c64[:, 0:H], hh[:, 0:H], A.add, A.min, ["c64", "hh%d" % rd], ["hw"])
+        ts(T.oh[:, 0:3], T.hw[:, 15::16], T.pf[:, 10:11], A.add, ["hw", "pf9"], ["oh"])
         for t in range(4):
-            (cp if t < 2 else act)(T.bb[:, t:4 * H:4], T.xp[:, C * t:C * t + C].indirect(T.oh[:, 0:3]), [xpk(t), "oh", "bb0"], ["bb"], grp=n_ + "bb")
+            out, src2 = T.bb[:, t:4 * H:4], T.x2[:, C * t:C * t + C].indirect(T.oh[:, 0:3])
+            if t < 2:
+                ts(out, src2, 0.5, A.mult, ["x2", "oh", "bb0"], ["bb"], grp=n_ + "bb")
+            else:
+                act(out, src2, ["x2", "oh", "bb0"], ["bb"], 0.5, n_ + "bb")
         lq, ls = T["lq%d" % rd], T["ls%d" % rd]
         qz(lq, ls, own, own + 128, T.bb[:], ["bb", "bb0"], ["own%d" % rd])
         for buf, view in ((lq, u8), (ls, lambda ap: ap)):
@@ -398,42 +403,43 @@ def rank_program(g, core, T, topo):
                ["own%d" % rd], ["sent%d" % rd], n_ + "send", fixed=("sent", 2 * lanes * (rd + 1)))
         op("X", None, [], ["land%d" % rd], n_ + "land", fixed=("arr%d" % rd, 2 * lanes * (N - 1)))
         if rd == 0:
-            late_constants_c()
-            act(T.c2r[:, 0:C], T.plc[:, 0:S_].indirect(T.oa0[:]), ["plc", "oa0"], ["c2r0"])
-            act(T.c2r[:, C:2 * C], T.c2r[:, 0:C], ["c2r0"], ["c2r"])
-            act(T.xh[:], T.xp[:], xps, ["xh"], 0.5)
+            for t in range(4):
+                act(T.xh[:, C * t:C * t + C], T.x0[:, t::4], ["x0"], ["xh"], 0.5, "xh")
             tt(T.fl[:], ps(3, C), T.h16[:], A.is_gt, ["h16"], ["fla", "flb", "ps3"])
-            qz(T.qe, T.se, 0, 512, T.ee[:], ["ee", "ee1"], ["qe"])
+            qz(T.qe, T.se, 0, 512, T.ee[:], ["ee0", "ee1", "ee2", "ee3"], ["qe"])
+            for k in range(2):
+                scan(T.aw[:, C * k:C * k + C], T.c16[:], T.ar[:, C * k:C * k + C], A.add, A.min, ["c16", "ar"], ["aw%d" % k])
         scan(T.fs[:], T.fl[:], T.e1[:], A.max, A.mult, ["fla", "flb", "e1"], ["fs"])
-        tt(T.pw[:], T.fs[:, 15::16], T.c0p[:], A.add, ["fs", "c0p"], ["pw"])
-        cp(T.op[:], T.pw[:], ["pw"], ["op"])
-        tt(T.am[:], T.c2r[:].indirect(T.op[:]), T.m16[:], A.mult, ["c2r", "c2r0", "op", "m16"], ["am"])
-        scan(T.aw[:], T.r16[:], T.am[:], A.mult, A.add, ["r16", "am"], ["aw"])
-        tt(T.da[:], T.aw[:, 15::16], T.a0[:], A.subtract, ["aw", "a0"], ["da"])
-        cp(T.oa1[:], T.aw[:, 15::16], ["aw"], ["oa1"])
-        ts(T.db[:], T.da[:], float(S_ - 256), A.is_ge, ["da"], ["db"], -float(S_), A.mult)
-        tt(T.e2[:, 15::16], T.da[:], T.db[:], A.add, ["da", "db"], ["e2"])
+        if rd == 0:
+            ts(T.b0[:], T.aw[:, 15:C:16], T.pf[:, 9:10], A.add, ["aw0", "pf9a"], ["b0"])
+            tt(T.nd[:], T.aw[:, 15:C:16], T.aw[:, C + 15::16], A.subtract, ["aw0", "aw1"], ["nd"])
+            tt(T.b1[:], T.b0[:], T.a0[:], A.subtract, ["b0", "a0"], ["b1"])
+        tt(T.t1[:], T.fs[:, 15::16], T.nd[:], A.mult, ["fs", "nd"], ["t1"])
         if last:
             qz(T.qv, T.sv, 0, 128, T.vt[:], ["vt"], ["qv"])
+        tt(T.da[:], T.t1[:], T.b1[:], A.add, ["t1", "b1"], ["da"])
+        tt(T.a1[:], T.t1[:], T.b0[:], A.add, ["t1", "b0"], ["a1"])
+        ts(T.db[:], T.da[:], float(S_ - 256), A.is_ge, ["da"], ["db"], -float(S_), A.mult)
+        cp(T.oa1[:], T.a1[:], ["a1"], ["oa1"])
+        tt(T.e2[:, 15::16], T.da[:], T.db[:], A.add, ["da", "db"], ["e2"])
         for b in range(4):
             mx(4 + b, T.qe, T.se, 128 * b, lq, ls, 0, S_, True, True, ["qe", "own%d" % rd, "land%d" % rd])
         dma("Y", T.hl[:, H * rd:H * rd + H], hh[0:128:16, 0:H], ["hh%d" % rd, "land%d" % rd], ["out_hl%d" % rd])
         for b in range(4):
             if b == 0:
-                cp(T.fp[:, 0:S_], ps(4, S_), [], ["fp0", "ps4"])
+                ts(T.fp[:, 0:S_], ps(4, S_), 0.5, A.mult, [], ["fp0", "ps4"])
             else:
-                act(T.fp[:, S_ * b:S_ * b + S_], ps(4 + b, S_), [], ["fp%d" % b, "ps%d" % (4 + b)])
-        fwin, fkey = (lambda t: T.fp[:, S_ * t:S_ * t + S_]), (lambda t: "fp%d" % t)
+                act(T.fp[:, C * b:C * b + S_], ps(4 + b, S_), [], ["fp%d" % b, "ps%d" % (4 + b)], 0.5)
+        fwin, fkey = (lambda t: T.fp[:, C * t:C * t + S_]), (lambda t: "fp%d" % t)
         (a0, a1), (b0, b1) = CH
-        z0 = product(T.z0, T.tg0, 0, C, fwin, fkey, lambda t: T.oa0[:], plane(T.xp, 0, C), ["oa0", xpk], A.mult,
+        z0 = product(T.z0, T.tg0, 0, C, fwin, fkey, lambda t: T.oa0[:], plane(T.x2, 0, C), ["oa0", "x2"], A.mult,
                      ["z0a", "z0b"], SC[0], n_ + "cz0")
-        z1a = product(T.z1, T.tg1, a0, a1, fwin, fkey, lambda t: T.oa1[:, a0 // 16:a1 // 16], plane(T.xp, a0, a1),
-                      ["oa1", xpk], A.mult, ["z1a"], SC[1], n_ + "cz1a")
-        z1b = product(T.z1, T.tg1, b0, b1, fwin, fkey, lambda t: T.oa1[:, b0 // 16:b1 // 16], plane(T.xp, b0, b1),
-                      ["oa1", xpk], A.mult, ["z1b"], SC[1], n_ + "cz1b")
+        z1a = product(T.z1, T.tg1, a0, a1, fwin, fkey, lambda t: T.oa1[:, a0 // 16:a1 // 16], plane(T.x2, a0, a1),
+                      ["oa1", "x2"], A.mult, ["z1a"], SC[1], n_ + "cz1a")
+        z1b = product(T.z1, T.tg1, b0, b1, fwin, fkey, lambda t: T.oa1[:, b0 // 16:b1 // 16], plane(T.x2, b0, b1),
+                      ["oa1", "x2"], A.mult, ["z1b"], SC[1], n_ + "cz1b")
         for b in range(4):
-            for d in range(2):
-                act(T.fh[:, 2 * S_ * b + S_ * d:2 * S_ * b + S_ * d + S_], T.fp[:, S_ * b:S_ * b + S_], ["fp%d" % b], ["fh"], 0.5, n_ + "fh")
+            act(T.fp[:, C * b + S_:C * b + C], T.fp[:, C * b:C * b + S_], ["fp%d" % b], ["fh"], None, n_ + "fh")
 
         def score(a, b, s, bank):
             keys_ = ["qz1a", "qz1c"] if s == "a" else ["qz1b"]
@@ -449,7 +455,7 @@ def rank_program(g, core, T, topo):
             ]
 
         def mix(a, b, s):
-            return product(T.mm, T.tg0, a, b, lambda t: T.fh[:, 2 * S_ * t:2 * S_ * t + 2 * S_], lambda t: "fh",
+            return product(T.mm, T.tg0, a, b, plane(T.fp, 0, C), lambda t: "fh",
                            lambda t: T.oa[:, a // 16:b // 16], plane(T.xh, a, b), ["oa" + s, "xh"], A.add, ["mm" + s], SM, n_ + "mm" + s)
 
         def layer(a, b, s, banks):
@@ -474,30 +480,33 @@ def rank_program(g, core, T, topo):
             dma("S", T.y[:, a:b], T.ysb[:, a:b], ["ysb" + s], ["out_y" + s], "out")
 
         sa_, sb_ = steps(a0, a1, "a", 0), steps(b0, b1, "b", 1)
-        for f in z0:
-            f()
+        z0[0]()
+        z0[1]()
         z1a[0]()
+        z0[2]()
+        z0[3]()
+        z1b[0]()
         qz(T.qz, T.sz, 0, C, T.z0[:], ["z0a", "z0b"], ["qz0"])
         mx(0, T.qk, T.sk, 128, T.qz, T.sz, a0, a1 - a0, True, False, ["qz0"])
         mx(1, T.qk, T.sk, 128, T.qz, T.sz, b0, b1 - b0, True, False, ["qz0"])
         for f in z1a[1:]:
             f()
-        z1b[0]()
+        z1b[1]()
         score(a0, a1, "a", 0)
-        for f in z1b[1:]:
+        for f in z1b[2:]:
             f()
         sa_[0]()
         score(b0, b1, "b", 1)
         sa_[1]()
-        sa_[2]()
         sb_[0]()
-        sa_[3]()
+        sa_[2]()
         sb_[1]()
+        sa_[3]()
+        sb_[2]()
         ma = mix(a0, a1, "a")
         ma[0]()
-        sb_[2]()
-        ma[1]()
         sb_[3]()
+        ma[1]()
         mb = mix(b0, b1, "b")
         ma[2]()
         ma[3]()

from concourse.bass import DstId, RemoteDMATransfer
from concourse.mybir import dt, AluOpType, ActivationFunctionType

C, H, R, N = 384, 48, 2, 4
S_ = N * H
LV = 8
KB = 64
BIG = 1e29
KS, KL = 256.0, 2048.0
CH = ((0, 256), (256, 384))
SP, SC, SM = ((0, 3), (2, 3)), (2, 3), 2
ORDER = ("iajTbUkcVsdqefgh", "abecdfqgh")

BF, F32, I32, U16, Q8, U8 = "bfloat16", "float32", "int32", "uint16", "float8_e4m3fn_x4", "uint8"
_B = {
    BF: "x0 x1 xp xh x2 xi xq z0 z1 tg0 tg1 mm fp cst:1536 vt bb zb:512 wn:480 gg:2304 dd:1024 o128 n128 t128 d128 cw:128 ee:2048 "
        "c16 h16 c2r e1 e2 fl fs fs2:384 r64 cmp cs:256 eq ar aw:768 c64:64",
    F32: "ysb nc nu key kk:384 pf:12 lev one sa va:192 plc tbl:400 v1:96 v2 hw:48 kw hh0 hh1:64 "
         "v3 c2a c2b a0 a0p b0 b1 nd t1 a1 da db af:24",
    I32: "l1 lo hi i16:48 l2:24 pi:1 pa:4 ki:64",
    U16: "og:144 o1:192 o1p om:48 olb:12 onw:2 nw:32 ork oa0 oa1 oa:24 or2 oh:4",
    Q8: "qz:768 qm qx qk:384 qw qc qe:512 qv:128 qd:256 qq:192 lq0 lq1:272",
    U8: "sz:768 sm sx sk:384 sw sc se:512 sv:128 sd:256 sq:192 ls0 ls1:272",
}
SCRATCH = {"vals": ("sbuf", [128, 6, 3, 8], F32), "gt": ("sbuf", [128, 4, 768], BF), "tt": ("sbuf", [128, 4, 768], BF)}
for _d, _text in _B.items():
    _names = []
    for _w in _text.split():
        _names.append(_w.split(":")[0])
        if ":" in _w:
            for _n in _names:
                SCRATCH[_n] = ("sbuf", [128, int(_w.split(":")[1])], _d)
            _names = []
for _i in range(8):
    SCRATCH["ps%d" % _i] = ("psum", [128, 512], F32)
POOL = {"s": 132, "d": 14}
SEMAPHORES = ["%s%d" % (_k, _i) for _k in POOL for _i in range(POOL[_k])] + ["arr0", "arr1", "sent"]


def _emit(ops, queues, T):
    last_w, readers, known, groups, before = {}, {}, {}, {}, {}
    for i, o in enumerate(ops):
        groups.setdefault(o["grp"], []).append(i)
    for i, o in enumerate(ops):
        deps = set()
        for k in o["r"]:
            deps.update(last_w.get(k, ()))
        for k in o["w"]:
            held = before.setdefault((o["grp"], k), set())
            held.update(last_w.get(k, ()))
            held.update(readers.get(k, ()))
            deps.update(held)
        if o["eng"] == "P":
            deps = set(d for d in deps if ops[d]["eng"] != "P")
        kn = known.setdefault(o["eng"], set())
        need = set(ops[d]["grp"] for d in deps if ops[d]["grp"] != o["grp"])
        o["waits"] = []
        for gr in sorted(need, key=lambda a: -groups[a][-1]):
            if gr in kn:
                continue
            assert groups[gr][-1] < i, ("group not complete", gr, o["grp"])
            o["waits"].append(gr)
            kn.add(gr)
            for m in groups[gr]:
                kn |= ops[m]["kn"]
        o["kn"] = set(kn)
        for k in o["r"]:
            readers.setdefault(k, []).append(i)
        for k in o["w"]:
            last_w[k] = [d for d in last_w.get(k, ()) if ops[d]["grp"] == o["grp"]] + [i]
            readers[k] = [d for d in readers.get(k, ()) if ops[d]["grp"] == o["grp"]]
    used = set(gr for o in ops for gr in o["waits"])
    sem, count, owner, nxt = {}, {}, {}, {"s": 0, "d": 0}
    for i, o in enumerate(ops):
        gr = o["grp"]
        if gr in used and gr not in sem:
            if o["fixed"]:
                sem[gr] = o["fixed"]
                continue
            pool = "d" if o["inc"] == 16 else "s"
            while True:
                s = "%s%d" % (pool, nxt[pool] % POOL[pool])
                nxt[pool] += 1
                if all(p in ops[m]["kn"] for p in owner.get(s, ()) for m in groups[gr]):
                    break
            owner.setdefault(s, []).append(gr)
            count[s] = count.get(s, 0) + sum(ops[m]["inc"] for m in groups[gr])
            sem[gr] = (s, count[s])
    for o in ops:
        q = queues[o["eng"]]
        for gr in o["waits"]:
            q.wait_ge(T.sem[sem[gr][0]], sem[gr][1])
        if o["fn"] is not None:
            ins = o["fn"]()
            if o["grp"] in used and not o["fixed"]:
                ins.then_inc(T.sem[sem[o["grp"]][0]], o["inc"])


def rank_program(g, core, T, topo):
    me = T.rank_of(core)
    if me is None:
        return
    A, AF = AluOpType, ActivationFunctionType
    V, S, P, Y = g.vector, g.scalar, g.tensor, g.sync
    ops = []

    def op(eng, fn, r=(), w=(), grp=None, inc=1, fixed=None):
        ops.append({"eng": eng, "fn": fn, "r": list(r), "w": list(w), "inc": inc, "fixed": fixed,
                    "grp": grp if grp is not None else "#%d" % len(ops)})

    def ts(out, in0, s1, o0, r, w, s2=None, o1=None, grp=None):
        if o1 is None:
            op("V", lambda: V.tensor_scalar(out, in0, s1, None, o0), r, w, grp)
        else:
            op("V", lambda: V.tensor_scalar(out, in0, s1, s2, o0, o1), r, w, grp)

    def tt(out, in0, in1, o, r, w, grp=None):
        op("V", lambda: V.tensor_tensor(out, in0, in1, o), r, w, grp)

    def cp(out, in_, r, w, grp=None):
        op("V", lambda: V.tensor_copy(out, in_), r, w, grp)

    def ms(ap, c, w, grp=None):
        op("V", lambda: V.memset(ap, c), (), w, grp)

    def scan(out, d0, d1, o0, o1, r, w):
        op("V", lambda: V.tensor_tensor_scan(out, d0, d1, 0.0, o0, o1), r, w)

    def qz(q, s, a, b, in_, r, w, grp=None):
        op("V", lambda: V.quantize_mx(q[:, a:b], s[:, a:b], in_), r, w, grp)

    def act(out, in_, r, w, scale=None, grp=None, bias=None, func=AF.Identity):
        if bias is not None:
            op("S", lambda: S.activation(out, in_, func, bias=bias, scale=scale), r, w, grp)
        elif scale is None:
            op("S", lambda: S.activation(out, in_, AF.Copy), r, w, grp)
        else:
            op("S", lambda: S.activation(out, in_, AF.Copy, scale=scale), r, w, grp)

    def mx(bank, lq, ls, a, rq, rs, b, n, start, stop, r, grp=None):
        op("P", lambda: P.matmul_mx(T["ps%d" % bank][:, 0:n], lq[:, a:a + 128], ls[:, a:a + 128],
                                    rq[:, b:b + n], rs[:, b:b + n], start, stop), r, ["ps%d" % bank], grp)

    def dma(eng, out, in_, r, w, grp=None):
        op(eng, lambda: (Y if eng == "Y" else S).dma_start(out, in_), r, w, grp, 16)

    def gp(fn, r, w):
        op("G", fn, r, w)

    def iota(out, pattern, base, r, w):
        gp(lambda: g.iota(out, pattern, base, 0, allow_small_or_imprecise_dtypes=True), r, w)

    def ps(b, n):
        return T["ps%d" % b][:, 0:n]

    def u8(ap):
        return ap.bitcast(dt.uint8)

    dma("Y", T.l1[:], T.c1[:], [], ["l1"])
    dma("Y", T.x0[:], T.x[:], [], ["x0"])
    dma("Y", T.x1[:], T.x[:], [], ["x1"])
    dma("Y", T.l2[:], T.c2[:], [], ["l2"])

    gp(lambda: g.iota(T.pi[:], [[0, 1]], 0, 1), [], ["pi"])
    ms(T.o128[:], 1.0, ["o128"])
    ms(T.wn[:, 0:160], 1.0, ["wn0"])
    ms(T.zb[:], 0.0, ["zb"])
    gp(lambda: g.affine_select(T.wn[:, 0:160], T.wn[:, 0:160], [[-1, 160]], A.is_equal, 0.0, 16, 1), ["wn0"], ["wn0"])
    gp(lambda: g.affine_select(T.o128[:], T.o128[:], [[-16, 8], [0, 16]], A.is_ge, 0.0, 0, 1), ["o128"], ["o128"])
    gp(lambda: g.affine_select(T.o128[:], T.o128[:], [[16, 8], [0, 16]], A.is_ge, 0.0, 15, -1), ["o128"], ["o128"])
    ts(T.pa[:, 0:1], T.pi[:], 128 - 16, A.bitwise_and, ["pi"], ["pa"], grp="pa")
    ts(T.pa[:, 1:2], T.pi[:], 15, A.bitwise_and, ["pi"], ["pa"], grp="pa")
    ts(T.pa[:, 2:3], T.pi[:], 128 - 32, A.bitwise_and, ["pi"], ["pa"], grp="pa")
    ms(T.r64[:], 1.0, ["r64"])
    cp(T.pf[:, 0:3], T.pa[:, 0:3], ["pa"], ["pf"])
    g16, pm = T.pf[:, 0:1], T.pf[:, 1:2]
    act(T.wn[:, 160:320], T.wn[:, 0:160], ["wn0"], ["wn"], -BIG, "wn", BIG)
    act(T.wn[:, 320:480], T.wn[:, 0:160], ["wn0"], ["wn"], BIG, "wn", -BIG)
    act(T.dd[:, 3::4], T.zb[:, 0:256], ["zb"], ["dd3"])
    act(T.n128[:], T.o128[:], ["o128"], ["n128"], -1.0)
    for a in range(4):
        ms(T.gt[:, a, 3::4], 0.0, ["gt3"], "fill")
    gp(lambda: g.affine_select(T.t128[:], T.n128[:], [[-1, 128]], A.is_gt, 0.0, 0, 1), ["n128"], ["t128"])
    gp(lambda: g.iota(T.i16[:], [[176, 2], [0, 24]], 0, 1), [], ["i16"])
    gp(lambda: g.affine_select(T.d128[:], T.t128[:], [[-1, 128]], A.not_equal, -512.0, 0, 1), ["t128"], ["d128"])
    iota(T.plc[:], [[1, 400]], 0, [], ["plc"])
    iota(T.lev[0:64, :], [[-1, LV], [0, 24]], LV - 1, [], ["lev"])
    iota(T.lev[64:128, :], [[1, LV], [0, 24]], 0, ["lev", "plc", "i16", "d128", "wn0", "pi"], ["lev2"])
    gp(lambda: g.affine_select(T.cw[:], T.zb[:, 0:128], [[-1, 128]], A.not_equal, 4.0 * KS, 0, 1), ["zb", "lev2"], ["cw0"])
    gp(lambda: g.affine_select(T.cw[:], T.cw[:], [[-1, 128]], A.not_equal, -KS, 1, 1), ["cw0"], ["cw"])
    for b in range(4):
        gp(lambda b=b: g.affine_select(T.ee[:, 512 * b:512 * b + 512], T.zb[:], [[-4, 128], [-1, 4]], A.not_equal, 1.0, b, 4),
           ["zb", "cw"], ["ee%d" % b])

    ts(T.lo[:], T.l1[:], 15, A.bitwise_and, ["l1"], ["lohi"], grp="lohi")
    ts(T.hi[:], T.l1[:], 4, A.logical_shift_right, ["l1"], ["lohi"], grp="lohi")
    ms(T.r64[:, 0::64], 0.0, ["r64"])
    for y, (src, k, c) in enumerate(((T.lo, 0, 336), (T.lo, 1, 176), (T.hi, 0, 16), (T.hi, 0, 0), (T.hi, 1, 16), (T.hi, 1, 0))):
        ts(T.vals[:, y], src[:, 24 * k:24 * k + 24], g16, A.add, ["lohi", "pf"], ["vals"], float(c), A.add, grp="vals")
    ts(T.o1[:, 0:48], T.l1[:], 4.0, A.mult, ["l1"], ["o1"], grp="o1")
    for t in range(3):
        cp(T.og[:, 48 * t:48 * t + 48], T.vals[:, :, t, :], ["vals"], ["og%d" % t])
    for t in range(1, 4):
        ts(T.o1[:, 48 * t:48 * t + 48], T.l1[:], 4.0, A.mult, ["l1"], ["o1"], float(t), A.add, grp="o1")
    for t in range(4):
        act(T.cst[:, t:512:4], T.o128[:], ["o128"], ["cst0"], None, "cst0")
    ts(T.cst[:, 512:1024], T.cst[:, 0:512], -1.0, A.mult, ["cst0"], ["cst1"])
    for t in range(3):
        act(T.gg[:, 768 * t:768 * t + 768], T.wn[:].indirect(T.og[:, 48 * t:48 * t + 48]), ["wn", "wn0", "og%d" % t], ["gg%d" % t])

    def turns(t):
        for a in range(4):
            op("V", lambda a=a: V.transpose(T.gt[:, a, t::4], T.gg[:, 768 * t + a:768 * t + 768:4]),
               ["gg%d" % t, "gt3"], ["gt%d" % t], "tr%d" % t)

    def shuffles():
        for a in range(4):
            dma("Y", T.tt[:, a, :], T.gt[32 * a:32 * a + 32, :, :], ["gt0", "gt1", "gt2", "gt3"], ["tt"], "tt")
        dma("Y", u8(T.qw[:]), T.wc[:], ["tt"], ["qw"], "ldw")
        dma("Y", T.sw[:], T.ws[:], [], ["qw"], "ldw")
        dma("Y", T.vt[:], T.v[:], [], ["vt"])

    def columns(i):
        if i == 0:
            ts(T.pf[:, 8:9], T.pf[:, 2:3], 64.0, A.is_ge, ["pf"], ["pf8"], -64.0, A.mult, grp="pf8")
            ts(T.pf[:, 4:5], pm, 8.0, A.is_ge, ["pf"], ["pf8"], grp="pf8")
            ts(T.pf[:, 9:10], pm, 15.0, A.not_equal, ["pf"], ["pf9a"], KS, A.mult, grp="pf8")
        elif i == 1:
            ts(T.pf[:, 7:8], T.pf[:, 2:3], 3.0, A.mult, ["pf", "pf8"], ["pf5"], T.pf[:, 8:9], A.add, grp="pf5")
            ts(T.pf[:, 5:6], T.pf[:, 4:5], -40.0, A.mult, ["pf8"], ["pf5"], 32.0, A.add, grp="pf5")
            ts(T.pf[:, 6:7], T.pf[:, 4:5], 16.0, A.mult, ["pf8"], ["pf5"], 8.0, A.add, grp="pf5")
        elif i == 2:
            ts(T.pf[:, 3:4], g16, T.pf[:, 7:8], A.add, ["pf", "pf5"], ["pf3"], pm, A.add)
            cp(T.om[:], T.i16[:], ["i16"], ["om"])

    def late_constants_a():
        zer = T.zb[:, 0:4]
        qz(T.qk, T.sk, 256, 384, T.cst[:, 1024:1536], ["cst3", "cst2"], ["qk2"])
        ts(T.olb[:, 0:12:3], zer, T.pf[:, 3:4], A.add, ["pf3", "zb"], ["olb"], grp="olb")
        ts(T.olb[:, 1:12:3], zer, T.pf[:, 3:4], A.add, ["pf3", "pf5", "zb"], ["olb"], T.pf[:, 5:6], A.add, grp="olb")
        ts(T.olb[:, 2:12:3], zer, T.pf[:, 3:4], A.add, ["pf3", "pf5", "zb"], ["olb"], T.pf[:, 6:7], A.add, grp="olb")
        ts(T.onw[:, 0:1], T.pf[:, 3:4], 0.0, A.add, ["pf3"], ["onw"], grp="olb")
        ts(T.onw[:, 1:2], T.pf[:, 3:4], 32.0, A.add, ["pf3"], ["onw"], grp="olb")

    def late_constants_c():
        ts(T.c2a[:], T.l2[:], float(S_ - H * (me + 1)), A.add, ["l2"], ["c2a"])
        cp(T.o1p[:], T.l1[:], ["l1"], ["o1p"])
        ts(T.c2b[:], T.c2a[:], float(S_), A.is_ge, ["c2a"], ["c2b"], -float(S_), A.mult)

    peers = [c for c in T.cores if c != core]
    mask = topo.mask(core, peers[0])
    for c in peers[1:]:
        mask &= topo.mask(core, c)
    lanes = bin(mask).count("1")
    ids = [DstId(rid=topo.addr(c)[0], pnc=topo.addr(c)[1]) for c in peers]
    spot = [H * ((me - T.rank_of(c) - 1) % N) for c in peers]
    own = H * (N - 1)

    def product(z, tg, a, b, win, wkey, off, other, okeys, alu, zk, split, name):
        tk = lambda t: ["%s%d%s" % (tg.name, t, k[-1]) for k in zk]
        ok = lambda t: [k if isinstance(k, str) else k(t) for k in okeys]
        for t in range(4 - split, 4):
            act(tg[:, C * t + a:C * t + b], win(t).indirect(off(t)), [wkey(t), okeys[0]], tk(t))
        out = []
        for t in range(4):
            if t < 4 - split:
                out.append(lambda t=t: tt(z[:, 4 * a + t:4 * b:4], win(t).indirect(off(t)), other(t), alu, [wkey(t)] + ok(t), zk, name))
            else:
                out.append(lambda t=t: tt(z[:, 4 * a + t:4 * b:4], tg[:, C * t + a:C * t + b], other(t), alu, tk(t) + ok(t)[1:], zk, name))
        return out

    def plane(buf, a, b):
        return lambda t: buf[:, C * t + a:C * t + b]

    xpk, xps = (lambda t: "xp%d" % t), ["xp%d" % t for t in range(4)]
    for rd in range(R):
        n_ = "r%d" % rd
        last = rd == R - 1
        if rd == 0:
            qz(T.qk, T.sk, 0, 256, T.cst[:, 0:1024], ["cst0", "cst1"], ["qk"])
            sk, nq = (lambda t: "x0"), 0
        else:
            sk, nq = xpk, 4 - min(SP[rd])
        for t in range(1, nq):
            act(T.xq[:, C * t:C * t + C], T.xp[:, C * t:C * t + C], [sk(t)], ["xq%d" % t])
        w = []
        for k, (z, tg) in enumerate(((T.z0, T.tg0), (T.z1, T.tg1))):
            zk = ["z%da" % k, "z%db" % k]
            if rd == 0:
                win, off = (lambda t: T.x0[:]), (lambda t, k=k: T.o1[:, 48 * t + 24 * k:48 * t + 24 * k + 24])
                oth, oks = (lambda t: T.x1[:, t::4]), ["o1", "x1"]
            else:
                win, off = plane(T.xp, 0, C), (lambda t, k=k: T.o1p[:, 24 * k:24 * k + 24])
                oth = lambda t, nq=nq: (T.xq if t < nq else T.xp)[:, C * t:C * t + C]
                oks = ["o1p", lambda t, nq=nq: ("xq%d" if t < nq else "xp%d") % t]
            w.append(product(z, tg, 0, C, win, sk, off, oth, oks, A.mult, zk, SP[rd][k], n_ + "pz%d" % k))
        step = dict(zip("abcdefgh", w[0] + w[1]))
        step.update(q=lambda: qz(T.qz, T.sz, 0, C, T.z0[:], ["z0a", "z0b"], ["qz0"]), s=shuffles,
                    T=lambda: turns(0), U=lambda: turns(1), V=lambda: turns(2),
                    i=lambda: columns(0), j=lambda: columns(1), k=lambda: columns(2))
        for c in ORDER[rd]:
            step[c]()
        for t in range(3):
            mx(t, T.qz, T.sz, 128 * t, T.qk, T.sk, 128, 128, True, False, ["qz0", "qk"])
        mx(3, T.qk, T.sk, 128, T.qz, T.sz, 0, C, True, False, ["qz0", "qk"])
        q1 = (["qz1a"], ["qz1c"], ["qz1b"])
        for t in range(3):
            qz(T.qz, T.sz, C + 128 * t, C + 128 * t + 128, T.z1[:, 512 * t:512 * t + 512], ["z1a", "z1b"], q1[t])
            mx(t, T.qz, T.sz, C + 128 * t, T.qk, T.sk, 0, 128, False, True, q1[t] + ["qk"])
        mx(3, T.qk, T.sk, 0, T.qz, T.sz, C, C, False, True, ["qz1a", "qz1b", "qz1c", "qk"])
        if rd == 0:
            act(T.cst[:, 1024:1536], T.zb[:], ["zb"], ["cst2"])
            act(T.eq[:, 0:512], T.zb[:], ["zb"], ["eq0"], grp="fs")
            act(T.cst[:, 1024:1536:4], T.d128[:], ["d128", "cst2"], ["cst3"])
            act(T.eq[:, 512:768], T.zb[:, 0:256], ["zb"], ["eq0"], grp="fs")
            act(T.one[:], T.zb[:, 0:192], ["zb"], ["one"], 1.0, "fs", 1.0)
            act(T.tbl[:], T.plc[:], ["plc"], ["tbl"], -512.0, None, float(C * 512))
            act(T.c16[:], T.cw[:].indirect(T.om[:, 0:24]), ["cw", "om"], ["c16"])
            act(T.h16[:], T.wn[:].indirect(T.om[:, 24:48]), ["wn", "wn0", "om"], ["h16"])
            act(T.bb[:], T.zb[:], ["zb"], ["bb0"])
            act(T.c64[:], T.c16[:, 0:KB], ["c16"], ["c64"], KL)
            act(T.pf[:, 10:11], T.pf[:, 9:10], ["pf9a"], ["pf9"], KL, "pf9")
            act(T.pf[:, 11:12], T.pf[:, 9:10], ["pf9a"], ["pf9"], -KL, "pf9")
            for a in range(4):
                qz(T.qc, T.sc, 128 * a, 128 * a + 128, T.tt[:, a, 256:768], ["tt"], ["qc"], "qc")
        else:
            act(T.x2[:], T.xp[:], xps, ["x2"], 2.0)
        for k, alu in enumerate((A.is_le, A.is_gt)):
            for t in range(3):
                tt(T.dd[:, 512 * k + t:512 * k + 512:4], ps(t, 128), T.tt[:, :, 128 * k + t:128 * k + 128:4], alu,
                   ["tt"], ["dd%d" % k, "ps%d" % t], n_ + "dd%d" % k)
            if rd == 0 and k == 0:
                late_constants_c()
            qz(T.qd, T.sd, 128 * k, 128 * k + 128, T.dd[:, 512 * k:512 * k + 512], ["dd%d" % k, "dd3"], ["qd%d" % k])
            mx(7, T.qd, T.sd, 128 * k, T.qc, T.sc, 256 + 64 * k, 192, k == 0, k == 1, ["qd%d" % k, "qc"])
            mx(4, T.qd, T.sd, 128 * k, T.qc, T.sc, 64 * k, 192, k == 0, k == 1, ["qd%d" % k, "qc"])
        if rd == 0:
            late_constants_a()
            tt(T.a0[:], T.c2a[:], T.c2b[:], A.add, ["c2a", "c2b"], ["a0"])
        else:
            tt(T.fl[:], ps(3, C), T.h16[:], A.is_gt, ["h16"], ["fla", "flb", "ps3"])
        ts(T.nc[:, 0:192], ps(4, 192), float(LV - 1), A.min, [], ["nc", "ps4"])
        act(T.nc[:, 192:384], ps(7, 192), [], ["nc2", "ps7"], -1.0, None, float(LV - 1), AF.Relu)
        act(T.nu[:, 192:384], ps(7, 192), [], ["nu", "ps7"], grp=n_ + "nu")
        act(T.nu[:, 0:192], ps(4, 192), [], ["nu", "ps4"], grp=n_ + "nu")
        if rd == 0:
            cp(T.oa0[:], T.a0[:], ["a0"], ["oa0"])
            act(T.c2r[:], T.plc[:, 0:S_].indirect(T.oa0[:]), ["plc", "oa0"], ["c2r"])
            for t in range(4):
                act(T.x2[:, C * t:C * t + C], T.x0[:, t::4], ["x0"], ["x2"], 2.0, "x2")
            act(T.ar[:], T.c2r[:].indirect(T.o1p[:]), ["c2r", "o1p"], ["ar"])
            act(T.e1[:], T.zb[:, 0:C], ["zb"], ["e1"], 1.0, None, 1.0)
            act(T.e2[:], T.zb[:, 0:C], ["zb"], ["e2"], 1.0, None, 1.0)
            act(T.e1[:, 15::16], T.zb[:, 0:24], ["zb"], ["e1"], 1.0, None, -1.0)
            act(T.a0p[:], T.a0[:], ["a0"], ["a0p"], 1.0, None, float(S_))
        else:
            act(T.xh[:], T.xp[:], xps, ["xh"], 0.5)
        tt(T.eq[:, 0::4], T.nc[:].indirect(T.olb[:]), T.lev[:], A.is_equal, ["nc", "nc2", "olb", "lev", "lev2", "eq0"], ["eq"])
        qz(T.qq, T.sq, 0, 192, T.eq[:], ["eq", "eq0"], ["qq"])
        mx(5, T.qk, T.sk, 0, T.qq, T.sq, 0, 192, True, True, ["qq", "qk"])
        mx(6, T.qk, T.sk, 256, T.qq, T.sq, 0, 192, True, True, ["qq", "qk2"])
        cp(T.nw[:], T.nu[:].indirect(T.onw[:]), ["nu", "onw"], ["nw"])
        scan(T.sa[:], T.one[:], ps(5, 192), A.mult, A.add, ["one"], ["sa", "ps5"])
        third = C // 3

        def keys(i):
            tt(T.key[:, third * i:third * i + third], T.tbl[:].indirect(T.nw[:, 8 * i:8 * i + 8]), T.plc[:, third * i:third * i + third],
               A.add, ["tbl", "nw", "plc"], ["key"], n_ + "key")

        keys(0)
        tt(T.va[:], T.sa[:], ps(6, 192), A.add, ["sa"], ["va", "ps6"])
        keys(1)
        tt(T.v1[:], T.va[:, 0:96], T.va[:, 96:192], A.min, ["va"], ["v1"])
        keys(2)
        tt(T.v2[:], T.v1[:, 0:48], T.v1[:, 48:96], A.min, ["v1"], ["v2"])
        tt(T.v3[:], T.v2[:, 0:24], T.v2[:, 24:48], A.min, ["v2"], ["v3"])
        ts(T.ork[:], T.v3[:], 511.0, A.add, ["v3"], ["ork"])
        cp(T.kk[:].indirect(T.ork[:]), T.key[:], ["ork", "key"], ["kk"])
        hh = T["hh%d" % rd]
        scan(T.kw[:], T.c64[:], T.kk[:, 0:KB], A.add, A.min, ["c64", "kk"], ["kw"])
        cp(T.ki[:], T.kk[:, 0:KB], ["kk"], ["ki"])
        for m in range(4):
            ts(T.cmp[:, KB * m:KB * m + KB], T.kk[:, 0:KB], T.pf[:, 11:12], A.add, ["kk", "kw", "pf9"], ["cmp"],
               T.kw[:, 16 * m + 15:16 * m + 16], A.is_lt, grp=n_ + "cmp")
        ts(T.ki[:], T.ki[:], 511, A.bitwise_and, ["ki"], ["ki"])
        scan(T.cs[:], T.r64[:], T.cmp[:], A.mult, A.add, ["r64", "cmp"], ["cs"])
        cp(T.or2[:], T.cs[:, KB - 1::KB], ["cs"], ["or2"])
        cp(hh[:].indirect(T.or2[:]), T.ki[:], ["or2", "ki"], ["hh%d" % rd])
        scan(T.hw[:], T.c64[:, 0:H], hh[:, 0:H], A.add, A.min, ["c64", "hh%d" % rd], ["hw"])
        ts(T.oh[:, 0:3], T.hw[:, 15::16], T.pf[:, 10:11], A.add, ["hw", "pf9"], ["oh"])
        for t in range(4):
            out, src2 = T.bb[:, t:4 * H:4], T.x2[:, C * t:C * t + C].indirect(T.oh[:, 0:3])
            if t < 2:
                ts(out, src2, 0.5, A.mult, ["x2", "oh", "bb0"], ["bb"], grp=n_ + "bb")
            else:
                act(out, src2, ["x2", "oh", "bb0"], ["bb"], 0.5, n_ + "bb")
        lq, ls = T["lq%d" % rd], T["ls%d" % rd]
        qz(lq, ls, own, own + 128, T.bb[:], ["bb", "bb0"], ["own%d" % rd])
        for buf, view in ((lq, u8), (ls, lambda ap: ap)):
            op("G", lambda buf=buf, view=view, rd=rd: g.remote_dma_fused([RemoteDMATransfer(
                dst_ids=ids, dma_engine_mask=mask, remote_sem=T.sem["arr%d" % rd],
                srcs=[view(buf[:, own:own + H])], dsts=[view(buf[:, s:s + H]) for s in spot])], local_sem=T.sem.sent),
               ["own%d" % rd], ["sent%d" % rd], n_ + "send", fixed=("sent", 2 * lanes * (rd + 1)))
        op("X", None, [], ["land%d" % rd], n_ + "land", fixed=("arr%d" % rd, 2 * lanes * (N - 1)))
        if rd == 0:
            for t in range(4):
                act(T.xh[:, C * t:C * t + C], T.x0[:, t::4], ["x0"], ["xh"], 0.5, "xh")
            tt(T.fl[:], ps(3, C), T.h16[:], A.is_gt, ["h16"], ["fla", "flb", "ps3"])
            qz(T.qe, T.se, 0, 512, T.ee[:], ["ee0", "ee1", "ee2", "ee3"], ["qe"])
            for k in range(2):
                scan(T.aw[:, C * k:C * k + C], T.c16[:], T.ar[:, C * k:C * k + C], A.add, A.min, ["c16", "ar"], ["aw%d" % k])
        scan(T.fs[:], T.fl[:], T.e1[:], A.max, A.mult, ["fla", "flb", "e1"], ["fs"])
        if rd == 0:
            ts(T.b0[:], T.aw[:, 15:C:16], T.pf[:, 9:10], A.add, ["aw0", "pf9a"], ["b0"])
            tt(T.nd[:], T.aw[:, 15:C:16], T.aw[:, C + 15::16], A.subtract, ["aw0", "aw1"], ["nd"])
            tt(T.b1[:], T.b0[:], T.a0[:], A.subtract, ["b0", "a0"], ["b1"])
        tt(T.t1[:], T.fs[:, 15::16], T.nd[:], A.mult, ["fs", "nd"], ["t1"])
        if last:
            qz(T.qv, T.sv, 0, 128, T.vt[:], ["vt"], ["qv"])
        tt(T.da[:], T.t1[:], T.b1[:], A.add, ["t1", "b1"], ["da"])
        tt(T.a1[:], T.t1[:], T.b0[:], A.add, ["t1", "b0"], ["a1"])
        ts(T.db[:], T.da[:], float(S_ - 256), A.is_ge, ["da"], ["db"], -float(S_), A.mult)
        cp(T.oa1[:], T.a1[:], ["a1"], ["oa1"])
        tt(T.e2[:, 15::16], T.da[:], T.db[:], A.add, ["da", "db"], ["e2"])
        for b in range(4):
            mx(4 + b, T.qe, T.se, 128 * b, lq, ls, 0, S_, True, True, ["qe", "own%d" % rd, "land%d" % rd])
        dma("Y", T.hl[:, H * rd:H * rd + H], hh[0:128:16, 0:H], ["hh%d" % rd, "land%d" % rd], ["out_hl%d" % rd])
        for b in range(4):
            if b == 0:
                ts(T.fp[:, 0:S_], ps(4, S_), 0.5, A.mult, [], ["fp0", "ps4"])
            else:
                act(T.fp[:, C * b:C * b + S_], ps(4 + b, S_), [], ["fp%d" % b, "ps%d" % (4 + b)], 0.5)
        fwin, fkey = (lambda t: T.fp[:, C * t:C * t + S_]), (lambda t: "fp%d" % t)
        (a0, a1), (b0, b1) = CH
        z0 = product(T.z0, T.tg0, 0, C, fwin, fkey, lambda t: T.oa0[:], plane(T.x2, 0, C), ["oa0", "x2"], A.mult,
                     ["z0a", "z0b"], SC[0], n_ + "cz0")
        z1a = product(T.z1, T.tg1, a0, a1, fwin, fkey, lambda t: T.oa1[:, a0 // 16:a1 // 16], plane(T.x2, a0, a1),
                      ["oa1", "x2"], A.mult, ["z1a"], SC[1], n_ + "cz1a")
        z1b = product(T.z1, T.tg1, b0, b1, fwin, fkey, lambda t: T.oa1[:, b0 // 16:b1 // 16], plane(T.x2, b0, b1),
                      ["oa1", "x2"], A.mult, ["z1b"], SC[1], n_ + "cz1b")
        for b in range(4):
            act(T.fp[:, C * b + S_:C * b + C], T.fp[:, C * b:C * b + S_], ["fp%d" % b], ["fh"], None, n_ + "fh")

        def score(a, b, s, bank):
            keys_ = ["qz1a", "qz1c"] if s == "a" else ["qz1b"]
            qz(T.qz, T.sz, C + a, C + b, T.z1[:, 4 * a:4 * b], ["z1" + s], keys_)
            mx(bank, T.qk, T.sk, 0, T.qz, T.sz, C + a, b - a, False, True, keys_)

        def steps(a, b, s, bank):
            return [
                lambda: tt(T.fl[:, a:b], ps(bank, b - a), T.h16[:, a:b], A.is_gt, ["h16"], ["fl" + s, "ps%d" % bank]),
                lambda: scan(T.fs2[:, a:b], T.fl[:, a:b], T.e2[:, a:b], A.max, A.mult, ["fl" + s, "e2"], ["fs" + s]),
                lambda: tt(T.af[:, a // 16:b // 16], T.fs2[:, a + 15:b:16], T.a0p[:, a // 16:b // 16], A.add, ["fs" + s, "a0p"], ["af" + s]),
                lambda: cp(T.oa[:, a // 16:b // 16], T.af[:, a // 16:b // 16], ["af" + s], ["oa" + s]),
            ]

        def mix(a, b, s):
            return product(T.mm, T.tg0, a, b, plane(T.fp, 0, C), lambda t: "fh",
                           lambda t: T.oa[:, a // 16:b // 16], plane(T.xh, a, b), ["oa" + s, "xh"], A.add, ["mm" + s], SM, n_ + "mm" + s)

        def layer(a, b, s, banks):
            qz(T.qm, T.sm, a, b, T.mm[:, 4 * a:4 * b], ["mm" + s], ["qm" + s])
            for t in range(4):
                mx(banks[t], T.qw, T.sw, 128 * t, T.qm, T.sm, a, b - a, True, True, ["qw", "qm" + s])

        def state(a, b, s, banks, t, eng):
            out = T.xi[:, 4 * a + t:4 * b:4] if last else T.xp[:, C * t + a:C * t + b]
            wk = ["xi" + s if last else xpk(t), "ps%d" % banks[t]]
            grp = n_ + "st" + (s if last else str(t))
            if eng == "V":
                ts(out, ps(banks[t], b - a), 0.03125, A.mult, [], wk, grp=grp)
            else:
                act(out, ps(banks[t], b - a), [], wk, 0.03125, grp)

        def outputs(a, b, s, bank):
            qz(T.qx, T.sx, a, b, T.xi[:, 4 * a:4 * b], ["xi" + s], ["qx" + s])
            mx(bank, T.qv, T.sv, 0, T.qx, T.sx, a, b - a, True, True, ["qv", "qx" + s])
            dma("Y", T.oc[:, 4 * a:4 * b], u8(T.qx[:, a:b]), ["qx" + s], ["out_oc" + s], "out")
            act(T.ysb[:, a:b], ps(bank, b - a), [], ["ysb" + s, "ps%d" % bank])
            dma("S", T.y[:, a:b], T.ysb[:, a:b], ["ysb" + s], ["out_y" + s], "out")

        sa_, sb_ = steps(a0, a1, "a", 0), steps(b0, b1, "b", 1)
        z0[0]()
        z0[1]()
        z1a[0]()
        z0[2]()
        z0[3]()
        z1b[0]()
        qz(T.qz, T.sz, 0, C, T.z0[:], ["z0a", "z0b"], ["qz0"])
        mx(0, T.qk, T.sk, 128, T.qz, T.sz, a0, a1 - a0, True, False, ["qz0"])
        mx(1, T.qk, T.sk, 128, T.qz, T.sz, b0, b1 - b0, True, False, ["qz0"])
        for f in z1a[1:]:
            f()
        z1b[1]()
        score(a0, a1, "a", 0)
        for f in z1b[2:]:
            f()
        sa_[0]()
        score(b0, b1, "b", 1)
        sa_[1]()
        sb_[0]()
        sa_[2]()
        sb_[1]()
        sa_[3]()
        sb_[2]()
        ma = mix(a0, a1, "a")
        ma[0]()
        sb_[3]()
        ma[1]()
        mb = mix(b0, b1, "b")
        ma[2]()
        ma[3]()
        ba, bb_ = (2, 3, 4, 5), (6, 7, 0, 1)
        mb[0]()
        layer(a0, a1, "a", ba)
        for f in mb[1:]:
            f()
        layer(b0, b1, "b", bb_)
        if last:
            for t, e in enumerate("SSSV"):
                state(a0, a1, "a", ba, t, e)
            state(b0, b1, "b", bb_, 0, "V")
            outputs(a0, a1, "a", 2)
            for t in range(1, 4):
                state(b0, b1, "b", bb_, t, "V")
            outputs(b0, b1, "b", 3)
            for k in range(4):
                dma("Y", T.osc[4 * k:4 * k + 4, :], T.sx[32 * k:32 * k + 4, :], ["qxa", "qxb"], ["out_sc"], "out")
        else:
            for t in range(4):
                state(a0, a1, "a", ba, t, "S")
                state(b0, b1, "b", bb_, t, "V")
                if t == 1:
                    cp(T.xq[:, 0:C], T.xp[:, 0:C], ["xp0"], ["xq0"])
    op("Y", None, ["out_hl0", "out_hl1", "out_oca", "out_ocb", "out_ya", "out_yb", "out_sc"], [])
    op("G", None, ["sent%d" % (R - 1)], [])
    _emit(ops, {"V": V, "S": S, "P": P, "Y": Y, "G": g, "X": None}, T)
